import numpy as np, ml_dtypes
CORES = [10,34,74,98]
N = 4
BF = ml_dtypes.bfloat16
def gentries(a):
    return np.ascontiguousarray(a.reshape(8, 16, -1).transpose(0, 2, 1)).reshape(8, -1)
def gtable(e):
    e = np.asarray(e); return np.ascontiguousarray(e.reshape(8, -1, 16).transpose(0, 2, 1)).reshape(128, -1).astype(np.int32)
W, L, RO, PE, ES, LAST = 4096, 256, 4, 2, 1, 1
def names(rng): return rng.integers(0, W, (N, 8, L, 16))
def pack(x, s, z):
    return {"cont": np.ascontiguousarray(np.reshape(x, (N, 128, W))).astype(np.float32).astype(BF),
            "enz": np.stack([gtable(a.reshape(8, -1)) for a in s]), "subs": np.stack([gtable(a.reshape(8, -1)) for a in z])}
def setup_inputs(rng):
    x = np.where(rng.random((N, 8, 1, W)) < 0.3, 51 * rng.integers(0, 6, (N, 8, 16, W)), rng.integers(0, 256, (N, 8, 16, W)))
    s, z = names(rng), names(rng); u = rng.random((N, 8, L, 1))
    z = np.where((u < 0.15) & (rng.random(z.shape) < 0.3), s[..., 15:], z)
    z = np.where((u > 0.9) & (rng.random(z.shape) < 0.5), z[..., 7:8], z)
    return pack(x, s, z)
def setup_inputs_spread(rng):
    x = np.minimum((np.exp2(3 + 5.5 * rng.random((N, 8, 1, W))) * rng.random((N, 8, 16, W))).astype(np.int64), 255)
    e = rng.choice(np.array([1.0, 1.5, 2.0, 3.0, 4.0]), (N, 8, 1, 1))
    s = np.minimum((W * rng.random((N, 8, L, 16)) ** e).astype(np.int64), W - 1)
    z = W - 1 - np.minimum((W * rng.random((N, 8, L, 16)) ** e).astype(np.int64), W - 1)
    return pack(x, s, z)
def setup_inputs_ends(rng):
    x = 255 * (rng.random((N, 8, 16, W)) < rng.choice(np.array([0.0, 0.1, 0.3, 0.5, 0.7, 0.9, 1.0]), (N, 8, 1, W)))
    near = (np.arange(16)[:, None] == rng.integers(0, 16, (N, 8, 1, W))) & (rng.random((N, 8, 1, W)) < 0.3)
    x = np.where(near, np.where(x == 0, 1, 254), x)
    m = np.stack([np.concatenate([rng.permutation(np.array([0, 10, 6, 8, 7, 9, 12])), np.array([16])]) for q in range(N)])
    top = np.argsort(rng.random((N, 8, 16)), axis=-1) < m[..., None]
    x[..., W - 1] = np.where(top, 255, 0); x[..., 0] = np.where(top, 0, 255)
    x[:, 7, :, W - 2] = 255; x[:, 7, 15, W - 2] = 254; x[:, 7, :, 1] = 0; x[:, 7, 0, 1] = 1
    x[:, 7, :, W - 3] = 255; x[:, 7, 14:, W - 3] = 254
    sz = []
    for i in range(2):
        fr = rng.choice(np.array([1.0, 0.6]), (N, 8, L, 1))
        sz.append(np.where(rng.random((N, 8, L, 16)) < fr, (W - 1) * rng.integers(0, 2, (N, 8, L, 16)), names(rng)))
    s, z = sz; alt = np.where(np.arange(16) & 1 == 1, W - 1, 0)
    for a, b, c in ((L - 1, L - 2, L - 3), (0, 1, 2)):
        s[:, 7, a] = W - 1 - alt; z[:, 7, a] = W - 1; z[:, 7, a, 9] = W - 2; z[:, 7, a, 15] = W - 2
        s[:, 7, b] = alt; z[:, 7, b] = 0
        s[:, 7, c] = alt; z[:, 7, c] = W - 1
        z[:, 7, c, 5] = W - 31
    for i, (p1, p2) in enumerate(((6, 11), (1, 14), (0, 15))):
        for a in (L - 4 - i, 3 + i):
            s[:, 7, a] = W - 1 - alt; z[:, 7, a] = W - 1; z[:, 7, a, p1] = W - 2; z[:, 7, a, p2] = W - 3
    return pack(x, s, z)
def setup_inputs_corners(rng):
    B = W // 16; kind = rng.integers(0, 7, (N, 8, B))
    for q in range(N):
        g = rng.permutation(8); kind[q, g[0]] = 0; kind[q, g[1]] = 3
    opts = ([0, 2, 4], [0, 2, 4], [5, 7, 9, 11], [6, 7, 8, 9], [10, 11, 12, 13], [5, 6, 7, 9, 10], list(range(17)))
    cs = np.zeros((N, 8, B, 16), np.int64)
    for i, o in enumerate(opts): cs = np.where(kind[..., None] == i, rng.choice(np.array(o), cs.shape), cs)
    cs[..., 0] = np.where(kind == 1, rng.choice(np.array([1, 3, 5]), kind.shape), cs[..., 0])
    down = (np.argsort(rng.random((N, 8, B, 16, 16)), axis=-1) < cs[..., None]).transpose(0, 1, 2, 4, 3).copy()
    down[..., 0] &= ~np.all(down, axis=-1)
    st = rng.integers(1, 17, down.shape); v = np.zeros(down.shape, np.int64); cur = np.full(down.shape[:-1], 255)
    for k in range(32):
        v[..., k & 15] = cur; cur = np.where(down[..., k & 15], cur - st[..., k & 15], 255)
    x = np.ascontiguousarray(v.transpose(0, 1, 3, 2, 4)).reshape(N, 8, 16, W)
    blk = np.concatenate([np.argsort(rng.random((N, 8, B)), axis=-1) for i in range(2)], axis=-1)[..., :L]
    rot = np.where(np.arange(L) < B, 0, rng.integers(0, 16, (N, 8, L)))
    s = 16 * blk[..., None] + ((np.arange(16) + rot[..., None]) & 15)
    inv = np.argsort(rng.random((N, 8, W)), axis=-1); new = np.argsort(inv, axis=-1)
    x = np.take_along_axis(x, inv[:, :, None], 3); s = np.take_along_axis(new, s.reshape(N, 8, -1), 2).reshape(N, 8, L, 16)
    one = rng.choice(np.array([0, W - 1, W // 2, 5]), (N, 8, L, 1)); s = np.where(rng.random((N, 8, L, 1)) < 0.1, one, s)
    z = names(rng); zk = rng.integers(0, 7, (N, 8, L, 1)); p = np.arange(16); own = s[..., 15:]
    z = np.where((zk == 1) & (p == 15), own, z); z = np.where((zk == 2) & ((p == 0) | (p == 15)), own, z)
    z = np.where(zk == 3, own, z); z = np.where(zk == 4, s, z)
    z = np.where(zk == 5, (W - 1) * rng.integers(0, 2, z.shape), z); z = np.where((zk == 6) & (p == rng.integers(0, 16, zk.shape)), own, z)
    return pack(x, s, z)
def setup_inputs_ties(rng):
    lev = np.array([[0, 1, 254, 255], [3, 4, 5, 250]])[np.arange(8) & 1]
    x = np.take_along_axis(np.broadcast_to(lev[None], (N, 8, 4)), rng.integers(0, 4, (N, 8, 16 * W)), 2).reshape(N, 8, 16, W)
    pool = rng.integers(0, W, (N, 8, 24)); pool[..., 0] = 0; pool[..., 1] = W - 1
    s = np.take_along_axis(pool, rng.integers(0, 24, (N, 8, L * 16)), 2).reshape(N, 8, L, 16)
    z = np.take_along_axis(pool, rng.integers(0, 24, (N, 8, L * 16)), 2).reshape(N, 8, L, 16)
    u = rng.random((N, 8, L, 1)); z = np.where(u < 0.2, s, z); z = np.where(u > 0.85, z[..., 3:4], z)
    return pack(x, s, z)
def setup_inputs_full(rng):
    B = W // 16; kind = np.stack([rng.permutation(np.array([0, 0, 0, 1, 1, 2, 2, 2])) for q in range(N)]); kind[0, 7] = 1; kind[N - 1, 7] = 0
    k4 = kind[:, :, None, None]
    cs = np.where(k4 == 0, rng.choice(np.array([10, 12, 14]), (N, 8, B, 16)), rng.integers(6, 16, (N, 8, B, 16)))
    cs[..., 0] += ((kind[:, :, None] == 0) & (rng.random((N, 8, B)) < 0.5)).astype(np.int64)
    t1 = np.argsort(rng.random((N, 8, B, 16)), axis=-1); t2 = np.argsort(rng.random((N, 8, B, 16)), axis=-1)
    down = ((t1[..., :, None] + t2[..., None, :]) & 15) < cs[..., None, :]
    st = rng.integers(1, 17, down.shape); v = np.zeros(down.shape, np.int64); cur = np.full(down.shape[:-1], 255)
    for k in range(32):
        v[..., k & 15] = cur; cur = np.where(down[..., k & 15], cur - st[..., k & 15], 255)
    x = np.ascontiguousarray(v.transpose(0, 1, 3, 2, 4)).reshape(N, 8, 16, W)
    blk = np.concatenate([np.argsort(rng.random((N, 8, B)), axis=-1) for i in range(2)], axis=-1)[..., :L]
    s = 16 * blk[..., None] + np.arange(16)
    inv = np.argsort(rng.random((N, 8, W)), axis=-1); new = np.argsort(inv, axis=-1)
    x = np.take_along_axis(x, inv[:, :, None], 3); s = np.take_along_axis(new, s.reshape(N, 8, -1), 2).reshape(N, 8, L, 16)
    hi = np.arange(W - 96, W); ok = ((hi[:, None] * np.arange(W) >> 5) & (W - 1)) + hi[:, None] + 77 == 2 * W
    made = np.where(np.any(ok, axis=1), np.argmax(ok, axis=1), -1); y = W - 32 + ((-((hi & 31) ** 7)) & 31)
    mate = np.full(W, -1); mate[W - 96:] = np.where(((hi & 1) == 1) & (hi * (y + 32) > 2 ** 24), y, made)
    zu = np.where(mate[s] >= 0, mate[s], names(rng)); zu[..., 0] = s[..., 15]
    way = 1 - 2 * (np.take_along_axis(cs[..., 0], blk, 2) & 1)
    p = (rng.integers(0, 16, (N, 8, L, 1)) + way[..., None] * np.arange(16)) & 15
    z = np.take_along_axis(zu, np.argsort(p, axis=-1), 3)
    z = np.where(rng.random((N, 8, L, 1)) < 0.75, z, names(rng))
    pm = np.argsort(rng.random((N, 8, W)), axis=-1); cl = (np.argsort(pm, axis=-1) >> 9)[:, :, None]
    few = rng.integers(0, 4, (N, 8, 16, W)); x2 = rng.integers(0, 256, (N, 8, 16, W)); x2 = np.where(cl == 0, few, x2)
    for i, b in ((1, 134), (2, 198), (3, 255)): x2 = np.where(cl == i, b - few, x2)
    s2 = names(rng); s2[..., 15] = np.take_along_axis(pm, rng.integers(0, 512, (N, 8, L)), 2)
    zi = 512 * rng.integers(1, 4, (N, 8, L, 1)) + rng.integers(0, 512, (N, 8, L, 16))
    z2 = np.take_along_axis(pm, zi.reshape(N, 8, -1), 2).reshape(N, 8, L, 16)
    return pack(np.where(k4 == 2, x2, x), np.where(k4 == 2, s2, s), np.where(k4 == 2, z2, z))
def check_inputs(d):
    bad = []
    c = np.asarray(d["cont"]).astype(np.float32)
    if not np.all((c >= 0) & (c <= 255)): bad.append("range of cont")
    elif not np.all(c == np.floor(c)): bad.append("whole numbers in cont")
    for k in ("enz", "subs"):
        if np.min(d[k]) < 0 or np.max(d[k]) > W - 1: bad.append("range of " + k)
    return bad
def edit(x, s, z, a, t):
    v = np.take_along_axis(x, s.reshape(8, 1, -1), 2).reshape(8, 16, L, 16)
    y = np.take_along_axis(x, z.reshape(8, 1, -1), 2).reshape(8, 16, L, 16)
    c = np.sum((v > np.roll(v, -1, axis=3)).astype(np.int64), axis=1)
    dist = np.sum(np.abs(y - v[..., 15:16]).astype(np.int64), axis=1)
    step = 1 - 2 * (np.add.accumulate(c, axis=2) & 1); step[..., 0] = np.argmin(dist, axis=2)
    pos = np.add.accumulate(step, axis=2) & 15
    hit = pos[:, :, None, :] == np.arange(16)[:, None]
    e = 15 - np.argmax(hit[..., ::-1], axis=3) if LAST else np.argmax(hit, axis=3)
    has = np.any(hit, axis=3); ce = np.take_along_axis(c, e, 2); se = np.take_along_axis(s, e, 2)
    gone = has & (ce <= 5 + (a & 1)[..., None])
    new = np.where(has, np.where(ce <= 9, se, ((se * z >> 5) + se + 77 * t) & (W - 1)), z)
    n = np.sum(gone.astype(np.int64), axis=2); i = np.arange(16) - (16 - n)[..., None]
    kept = np.take_along_axis(new, np.argsort(gone, axis=2, kind="stable"), 2)
    return np.where(i < 0, kept, np.take_along_axis(s, np.maximum(i, 0), 2)), n
def reference(cont, enz, subs):
    x = cont.astype(np.float32).astype(np.int16).reshape(N, 8, 16, W)
    s = np.stack([gentries(a) for a in enz]).astype(np.int64).reshape(N, 8, L, 16)
    z = np.stack([gentries(a) for a in subs]).astype(np.int64).reshape(N, 8, L, 16)
    dels = np.zeros((N, 8, L), np.int64)
    for t in range(1, RO + 1):
        both = [edit(x[r], s[r], z[r], dels[r], t) for r in range(N)]
        dels = np.stack([b[1] for b in both])
        z = np.roll(s, ES, axis=0)
        s = np.roll(np.stack([b[0] for b in both]), PE, axis=0)
    return {"yenz": np.stack([gtable(a.reshape(8, -1)) for a in s]).astype(np.float32), "ysub": np.stack([gtable(a.reshape(8, -1)) for a in z]).astype(np.float32)}

@@ -1,0 +1,574 @@
+import math
+from concourse.mybir import AluOpType as A, ActivationFunctionType as AF
+
+RO, LH = 4, 128
+NH = 2
+SC = 1.0
+PC = 0.5
+GC = 1.55
+NET = 4000.0
+SCRATCH, SEMAPHORES = {}, []
+
+
+def _sb(name, cols, dtype="bfloat16"):
+    SCRATCH[name] = ("sbuf", [128, cols], dtype)
+
+
+F32, BF, I32, U16, F16 = "float32", "bfloat16", "int32", "uint16", "float16"
+_sb("ct", 4096)
+_sb("ei", 256, I32); _sb("zi", 256, I32)
+_sb("eo", 1280, U16); _sb("es", 1280, F32); _sb("zo", 1280, U16); _sb("zs", 1280, F32)
+_sb("po", 1024, U16); _sb("ps", 1024, F32)
+CB = {}
+for _n, _w in ([("I", 128), ("nI", 128), ("I128", 128), ("m127", 128), ("m128", 128), ("m4096", 128), ("m64", 128), ("p32", 128),
+               ("R128", 128), ("mR", 128), ("A1", 128), ("A2", 128), ("B1", 128), ("B2", 128), ("P1", 128), ("P2", 128), ("Sp", 128), ("tri", 128),
+               ("ones", 128), ("cC", 128), ("cD", 128), ("odd", 256), ("UU", 128), ("zero", 128), ("neg", 128), ("pos", 128), ("keep", 128),
+               ("b16", 16), ("b32", 16), ("bm16", 16)] + [("W%d" % k, 128) for k in range(16)]):
+    CB[_n] = (sum(w for _, w in CB.values()), _w)
+_sb("cb", sum(w for _, w in CB.values()))
+CF = {}
+for _n in ("IF", "RF", "DA", "DB", "TC", "TS", "IV"):
+    CF[_n] = (128 * len(CF), 128)
+_sb("cf", 128 * len(CF), F32)
+_sb("ch", 32, F16)
+_sb("b8", 8, F32)
+_sb("col", 16, F32)
+for _n, _w, _d in (("KI", 128, F32), ("KD", 128, F32), ("KV", 128, F32), ("KT", 128, F32), ("UM", 128, F32), ("GG", 128, F32), ("t1", 128, F32),
+                   ("t2", 128, F32), ("ki", 128, I32), ("pi", 2, I32), ("K8", 8, F32), ("u16f", 16, F32), ("f16", 16, F32), ("im16", 16, F32),
+                   ("n80", 80, F32), ("n80i", 80, I32), ("w80", 80, F32), ("x80", 80, F32), ("a80", 80, F32)):
+    _sb("k_" + _n, _w, _d)
+for _h in range(NH):
+    for _n, _w, _d in (("V", 2048, BF), ("Y", 2048, BF), ("cmp", 2048, BF), ("mx", 2048, BF), ("PA", 2048, F16), ("PB", 2048, F16), ("km", 128, F32),
+                       ("r8", 8, F32), ("E", 128, BF), ("q1", 128, BF), ("q2", 128, BF), ("r", 128, F32), ("X", 128, BF), ("Mx", 128, BF),
+                       ("Mn", 128, BF), ("LT", 384, BF), ("r16", 128, BF), ("hS", 128, BF), ("XA", 128, F16), ("XB", 128, F16), ("v", 128, I32),
+                       ("S", 128, I32), ("cd", 128, I32), ("q", 128, F32), ("Zq", 128, F32), ("pr", 128, I32), ("F", 128, I32), ("m2", 128, F32),
+                       ("val", 128, F32), ("del", 128, BF), ("E2", 128, BF), ("h2", 128, BF), ("EL", 128, BF), ("h", 128, BF), ("hf", 128, F32),
+                       ("AB", 256, F32), ("PP", 256, F32), ("fi", 128, F32), ("fm", 128, F32), ("w", 128, I32), ("pi", 128, I32), ("pf", 128, F32)):
+        _sb("%s%d" % (_n, _h), _w, _d)
+    for _n in "abcd":
+        SCRATCH["ps%s%d" % (_n, _h)] = ("psum", [128, 512], F32)
+SEMAPHORES += ["qP", "qV", "qS", "qG", "ld0", "ld1", "ld2", "snt", "out"]
+for _t in range(1, RO + 1):
+    for _h in range(NH):
+        SEMAPHORES += ["%s%d%d" % (_k, _t, _h) for _k in ("eo", "es", "zo", "zs")]
+
+
+def R(buf, c0, c1, step=1):
+    return (buf, c0, c1, step)
+
+
+def cb(n, lo=0, hi=None):
+    c, w = CB[n]
+    return R("cb", c + lo, c + (w if hi is None else hi))
+
+
+def cf(n):
+    c, w = CF[n]
+    return R("cf", c, c + w)
+
+
+def ap(T, r):
+    return T[r[0]][:, r[1]:r[2]:r[3]] if r[3] != 1 else T[r[0]][:, r[1]:r[2]]
+
+
+def ncol(r):
+    return (r[2] - r[1] + r[3] - 1) // r[3]
+
+
+def dts(r):
+    return SCRATCH[r[0]][2]
+
+
+def isp(r):
+    return SCRATCH[r[0]][0] == "psum"
+
+
+OPS = []
+
+
+def op(eng, dur, fns, reads, writes, sem=None, inc=1, dep=None):
+    OPS.append({"e": eng, "d": dur, "f": fns, "r": reads, "w": writes, "sem": sem, "inc": inc, "dep": dep})
+    return len(OPS) - 1
+
+
+def two(rs):
+    return all(dts(r) in (BF, F16, U16) and not isp(r) for r in rs)
+
+
+def cyc(n, x):
+    return max(64.0, n * x) * SC + 8.0
+
+
+def ts(out, a, s1, op0, s2=None, op1=None):
+    cols = [s for s in (s1, s2) if isinstance(s, tuple)]
+
+    def f(g, T):
+        x = ap(T, s1) if isinstance(s1, tuple) else s1
+        y = ap(T, s2) if isinstance(s2, tuple) else s2
+        if op1 is None:
+            return g.vector.tensor_scalar(ap(T, out), ap(T, a), x, None, op0)
+        return g.vector.tensor_scalar(ap(T, out), ap(T, a), x, y, op0, op1)
+    return op("V", cyc(ncol(out), 0.5 if two([out, a]) else 1), [f], [a] + cols, [out])
+
+
+def tt(out, a, b, o):
+    return op("V", cyc(ncol(out), 1 if isp(a) or isp(b) else 2), [lambda g, T: g.vector.tensor_tensor(ap(T, out), ap(T, a), ap(T, b), o)], [a, b], [out])
+
+
+def cp(out, a):
+    return op("V", cyc(ncol(out), 0.5 if two([out, a]) else 1), [lambda g, T: g.vector.tensor_copy(ap(T, out), ap(T, a))], [a], [out])
+
+
+def fill(out, c):
+    return op("V", cyc(ncol(out), 0.5), [lambda g, T: g.vector.memset(ap(T, out), c)], [], [out])
+
+
+def scan(out, d0, d1, o0, o1):
+    return op("V", cyc(ncol(out), 0.5 if two([out, d0, d1]) else 1),
+              [lambda g, T: g.vector.tensor_tensor_scan(ap(T, out), ap(T, d0), ap(T, d1), 0.0, o0, o1)], [d0, d1], [out])
+
+
+def act(out, a, func, bias=None):
+    def f(g, T):
+        if bias is None:
+            return g.scalar.activation(ap(T, out), ap(T, a), func)
+        return g.scalar.activation(ap(T, out), ap(T, a), func, bias=bias)
+    return op("S", ncol(out) * SC + 20, [f], [a], [out])
+
+
+def gather(eng, out, offs):
+    n = ncol(out)
+    if eng == "S":
+        f = lambda g, T: g.scalar.activation(ap(T, out), T["ct"][:, 0:4096].indirect(ap(T, offs)), AF.Copy)
+    else:
+        f = lambda g, T: g.vector.tensor_copy(ap(T, out), T["ct"][:, 0:4096].indirect(ap(T, offs)))
+    return op(eng, n * GC * SC + 60, [f], [R("ct", 0, 4096), offs], [out])
+
+
+def mm(lst):
+    fns, rd, wr, d = [], [], [], 0.0
+    for out, l, r, st, sp in lst:
+        fns.append(lambda g, T, out=out, l=l, r=r, st=st, sp=sp: g.tensor.matmul(ap(T, out), ap(T, l), ap(T, r), st, sp))
+        rd += [l, r]; wr.append(out)
+        d += max(64, ncol(r)) * PC * (4 if dts(l) == F32 else 1)
+    return op("P", d, fns, rd, wr)
+
+
+def group(out, terms):
+    return [(out, l, r, i == 0, i == len(terms) - 1) for i, (l, r) in enumerate(terms)]
+
+
+def iota(out, pattern, base, cm):
+    kw = {} if dts(out) == I32 else {"allow_small_or_imprecise_dtypes": True}
+    return op("G", 130 + 2 * ncol(out) * SC, [lambda g, T: g.iota(ap(T, out), pattern, base, cm, **kw)], [], [out])
+
+
+def constants():
+    K = lambda n, w: R("k_" + n, 0, w)
+    KI, KD, KV, KT, UM, GG, t1, t2 = [K(n, 128) for n in ("KI", "KD", "KV", "KT", "UM", "GG", "t1", "t2")]
+    ki, pi, K8 = K("ki", 128), K("pi", 2), K("K8", 8)
+    col = lambda j: R("col", j, j + 1)
+    iota(KI, [[-16, 8], [0, 16]], 0, 1)
+    iota(KD, [[1, 128]], 0, -1)
+    iota(K8, [[-16, 8]], 0, 1)
+    iota(KV, [[-16, 8], [1, 16]], 0, 1)
+    iota(UM, [[0, 8], [1, 16]], 0, 0)
+    iota(pi, [[0, 2]], 0, 1)
+    iota(KT, [[16, 8], [1, 16]], 0, -1)
+    for n, c in (("I", 1.0), ("nI", -1.0), ("I128", 1.0 / 128), ("m127", -127.0), ("m128", -128.0), ("m4096", -4096.0), ("m64", -64.0), ("p32", 32.0)):
+        ts(cb(n), KD, 0.0, A.is_equal, c, A.mult)
+    fill(cb("ones"), 1.0); fill(cb("zero"), 0.0)
+    for h in range(NH):
+        fill(R("E%d" % h, 0, 128), 0.0)
+    b8, t8 = R("b8", 0, 8), R("k_t1", 0, 8)
+    ts(t8, K8, 0.0, A.is_ge)
+    ts(b8, K8, 15.0, A.is_le)
+    tt(b8, b8, t8, A.mult)
+    for half in (0, 8):
+        ts(cb("b16", half, half + 8), b8, 1.0, A.mult)
+    ts(cb("b32", 0, 8), b8, 32.0, A.mult)
+    ts(cb("bm16", 0, 8), b8, -16.0, A.mult)
+    ts(R("ch", 0, 8), b8, 128.0, A.mult)
+    ts(R("ch", 16, 24), b8, 1.0, A.mult)
+    ts(GG, KI, 0.0, A.is_ge)
+    ts(t1, KI, 15.0, A.is_le)
+    tt(GG, GG, t1, A.mult)
+    ts(t1, UM, 7.5, A.subtract, 1.0 / 128, A.mult)
+    cp(cb("cD"), t1)
+    ts(cb("cC"), UM, 1.0, A.is_ge, -1.0 / 128, A.mult)
+    ts(cb("neg"), UM, 0.0, A.is_equal, -1000.0, A.mult)
+    ts(cb("pos"), UM, 0.0, A.is_equal, 1048576.0, A.mult)
+    ts(cb("keep"), UM, 1.0, A.is_ge)
+    ts(t1, UM, 1.0, A.is_ge)
+    tt(t1, t1, GG, A.mult)
+    ts(t1, t1, -99.0, A.mult, 99.0, A.add)
+    tt(cb("UU"), t1, UM, A.add)
+    for k in range(16):
+        ts(cb("W%d" % k), cb("UU"), 16.5 - k, A.is_le)
+    cp(ki, KI)
+    ts(ki, ki, 1, A.bitwise_and)
+    tt(t1, ki, GG, A.mult)
+    c0 = CB["odd"][0]
+    fill(R("cb", c0, c0 + 128), 0.0)
+    ts(R("cb", c0 + 128, c0 + 256), t1, -2.0, A.mult)
+    for w, a1, a2 in ((127.0, "A1", "A2"), (128.0, "B1", "B2"), (1.0, "P1", "P2")):
+        ts(cb(a2), KI, 15.0, A.is_equal, w, A.mult)
+        ts(t2, KD, 0.0, A.is_equal, w, A.mult)
+        tt(cb(a1), t2, cb(a2), A.subtract)
+    ts(t1, KD, 0.0, A.is_equal, 4096.0, A.mult)
+    ts(t2, KD, 1.0, A.is_equal, 4096.0, A.mult)
+    tt(t1, t1, t2, A.subtract)
+    ts(t2, UM, 1.0, A.is_ge)
+    tt(cb("Sp"), t1, t2, A.mult)
+    ts(cb("R128"), KV, 15.0, A.is_equal, 1.0 / 128, A.mult)
+    ts(cb("mR"), KV, 15.0, A.is_equal, -1.0, A.mult)
+    ts(cf("RF"), KV, 15.0, A.is_equal)
+    ts(cf("IF"), KD, 0.0, A.is_equal)
+    ts(t1, KT, 0.0, A.is_ge)
+    tt(cb("tri"), t1, GG, A.mult)
+    ts(pi, pi, 15, A.bitwise_and)
+    ri = col(0)
+    cp(ri, R("k_pi", 0, 1))
+    ts(col(1), ri, 1.0, A.is_ge, -4096.0, A.mult)
+    ts(col(2), col(1), 960.0 + 16512.0, A.add)
+    ts(col(1), col(1), 127 * 7.5 + 96 - 129, A.add)
+    ts(col(3), ri, 127.0, A.mult, -129.0, A.add)
+    ts(col(4), ri, 128.0, A.mult, 16512.0, A.add)
+    ts(col(5), ri, -1.0, A.mult, 16.0, A.add)
+    u, f16, im = K("u16f", 16), K("f16", 16), K("im16", 16)
+    cp(u, R("k_UM", 0, 16))
+    ts(im, u, 9.0, A.is_ge)
+    ts(f16, im, -8.0, A.mult)
+    tt(f16, f16, u, A.add)
+    ts(im, im, 4.0, A.mult)
+    ts(col(6), ri, 9.0, A.is_ge)
+    ts(col(7), col(6), -8.0, A.mult)
+    tt(col(7), col(7), ri, A.add)
+    ts(col(6), col(6), 4.0, A.mult)
+    ts(col(8), col(7), 0.0, A.is_equal)
+    ts(col(9), col(7), 8.0, A.is_equal)
+    tt(col(8), col(8), col(9), A.add)
+    ts(col(8), col(8), -1.0 / 16, A.mult, 2.0 / 16, A.add)
+    n = lambda j: R("k_n80", 16 * j, 16 * j + 16)
+    ts(n(2), f16, ri, A.mult)
+    tt(n(0), n(2), im, A.add)
+    ts(n(1), n(0), 4.0, A.add)
+    ts(n(3), n(2), 12.0, A.add)
+    ts(n(4), u, col(7), A.mult, col(6), A.add)
+    N, NI, W, X2, AC = K("n80", 80), K("n80i", 80), K("w80", 80), K("x80", 80), K("a80", 80)
+    cp(NI, N)
+    ts(NI, NI, 15, A.bitwise_and)
+    cp(N, NI)
+    ts(W, N, -1.0, A.mult, 16.0, A.add)
+    tt(W, W, N, A.min)
+    ts(W, W, -1.0, A.mult, 4.0, A.add)
+    tt(X2, W, W, A.mult)
+    cc = [(-1) ** k * (math.pi / 8) ** (2 * k + 1) / math.factorial(2 * k + 1) for k in range(7)]
+    ts(AC, X2, cc[6], A.mult, cc[5], A.add)
+    for k in (4, 3, 2, 1, 0):
+        tt(AC, AC, X2, A.mult)
+        ts(AC, AC, cc[k], A.add)
+    tt(AC, AC, W, A.mult)
+    iv = R("k_a80", 64, 80)
+    ts(iv, iv, col(8), A.mult)
+    for j, name in enumerate(("DA", "DB", "TC", "TS", "IV")):
+        c = CF[name][0]
+        for q in range(8):
+            ts(R("cf", c + 16 * q, c + 16 * q + 16), R("k_a80", 16 * j, 16 * j + 16), R("b8", q, q + 1), A.mult)
+
+
+M4, M16 = 1.5 * 2 ** 25, 1.5 * 2 ** 27
+
+
+def half_round(t, h, hop):
+    b = lambda n, lo=0, hi=128: R("%s%d" % (n, h), lo, hi)
+    pa, pb, pc, pd = ["ps%s%d" % (x, h) for x in "abcd"]
+    q = lambda p, j, k=1: R(p, 128 * j, 128 * (j + k))
+    o = 256 * (t - 1) + 128 * h
+    eo, es, zo, zs = R("eo", o, o + 128), R("es", o, o + 128), R("zo", o, o + 128), R("zs", o, o + 128)
+    col = lambda j: R("col", j, j + 1)
+    hop(t, h, "z")
+    gather("S", b("V", 0, 2048), eo)
+    gather("S", b("Y", 0, 2048), zo)
+    act(b("hS"), es, AF.Identity, 16448.5)
+    mm([(q(pd, 0), cb("I"), R("V%d" % h, 15, 2048, 16), True, True)])
+    for p in range(16):
+        tt(b("mx", 128 * p, 128 * p + 128), R("Y%d" % h, p, 2048, 16), q(pd, 0), A.max)
+    mm([(q(pd, 1), cb("ones"), cb("cD"), True, False)])
+    for p in range(16):
+        dst = R(pd, 128 + p, 256, 16)
+        mm([(dst, b("mx", 128 * p, 128 * p + 128), cb("b32", 0, 8), False, False),
+            (dst, R("Y%d" % h, p, 2048, 16), cb("bm16", 0, 8), False, p == 15)])
+    scan(b("km"), cb("pos"), q(pd, 1), A.add, A.min)
+    km = R("km%d" % h, 15, 128, 16)
+    ts(b("r8", 0, 8), km, M16, A.add, M16, A.subtract)
+    tt(R("E%d" % h, 15, 128, 16), km, b("r8", 0, 8), A.subtract)
+    for c in range(4):
+        bank = pa if c % 2 == 0 else pb
+        lst = []
+        for j in range(4):
+            k = 4 * c + j
+            lst += group(q(bank, j), [(cb("I"), R("V%d" % h, k, 2048, 16)), (cb("nI"), R("V%d" % h, (k + 1) % 16, 2048, 16))])
+        mm(lst)
+        act(b("cmp", 512 * c, 512 * c + 512), q(bank, 0, 4), AF.Sign, -0.5)
+    mm(group(q(pc, 0), [(cb("ones"), cb("cC"))] + [(b("cmp", 128 * k, 128 * k + 128), cb("W%d" % k)) for k in range(16)]))
+    mm([(q(pc, 1, 2), cb("zero") if t == 1 else b("h"), cb("odd"), True, False)] +
+       [(R(pc, 128 + 15 - k, 384, 16), b("cmp", 128 * k, 128 * k + 128), cb("b16"), False, k == 15) for k in range(16)])
+    ts(b("r"), q(pc, 0), M4, A.add, M4, A.subtract)
+    scan(b("X"), q(pc, 0), b("r"), A.add, A.subtract)
+    ts(b("q1"), q(pc, 2), -5.0, A.is_gt)
+    ts(b("q2"), q(pc, 1), 3.0, A.is_gt)
+    scan(b("Mx"), cb("neg"), b("X"), A.add, A.max)
+    scan(b("Mn"), cb("pos"), b("X"), A.add, A.min)
+    mm(group(q(pa, 0), [(b("Mx"), cb("I")), (b("Mn"), cb("nI"))]) + group(q(pa, 1), [(b("X"), cb("I"))]) + group(q(pa, 2), [(b("E"), cb("I"))]))
+    act(b("LT", 0, 384), q(pa, 0, 3), AF.Copy)
+    sp, X, E = b("LT", 0, 128), b("LT", 128, 256), b("LT", 256, 384)
+    mm(group(q(pb, 0), [(cb("P1"), X), (cb("P2"), E)]))
+    ts(b("r16"), q(pb, 0), M16, A.add, M16, A.subtract)
+    mm(group(q(pc, 0), [(cb("A1"), X), (cb("A2"), E), (cb("Sp"), sp), (b("q1"), cb("m64")), (b("q2"), cb("p32")), (cb("R128"), b("hS")), (cb("m127"), b("r16"))]) +
+       group(q(pc, 1), [(cb("B1"), X), (cb("B2"), E), (cb("Sp"), sp), (cb("mR"), b("hS")), (cf("RF"), es), (cb("m128"), b("r16"))]))
+    ts(b("XA"), q(pc, 0), col(1), A.add)
+    ts(b("XB"), q(pc, 1), col(2), A.add)
+    mm(group(q(pc, 2), [(cf("DA"), es)]) + group(q(pc, 3), [(cf("DB"), es)]))
+    act(b("AB", 0, 256), q(pc, 2, 2), AF.Copy)
+
+    def route(bank):
+        for p in range(16):
+            x, y = b("PA", 128 * p, 128 * p + 128), b("PB", 128 * p, 128 * p + 128)
+            ts(x, b("XA"), 127.0 * p, A.max, 127.0 * (p + 1), A.min)
+            ts(y, b("XB"), 128.0 * p, A.max, 128.0 * (p + 1), A.min)
+            mm(group(R(bank, p, 128, 16), [(x, R("ch", 0, 8)), (y, R("ch", 16, 24))]))
+
+    mm(group(q(pa, 0), [(zs, cf("IF"))]))
+    route(pd)
+    cp(b("v"), q(pd, 0))
+    ts(b("S"), b("v"), 4095, A.bitwise_and)
+    ts(b("cd"), b("v"), 12, A.arith_shift_right, 3, A.bitwise_and)
+    tt(b("pr"), b("S"), q(pa, 0), A.mult)
+    ts(b("del"), b("cd"), 3.0, A.is_ge)
+    ts(b("q"), b("cd"), 1.0, A.is_ge, -8192.0, A.mult)
+    ts(b("F"), b("pr"), 5, A.arith_shift_right, 4095, A.bitwise_and)
+    ts(b("m2"), b("cd"), 2.0, A.is_ge)
+    scan(b("E2"), cb("keep"), b("del"), A.mult, A.add)
+    tt(b("Zq"), b("q"), q(pa, 0), A.add)
+    ts(q(pa, 1), b("F"), 77.0 * t, A.add)
+    tt(q(pa, 2), b("m2"), q(pa, 1), A.mult)
+    tt(q(pa, 3), b("S"), q(pa, 2), A.add)
+    tt(b("val"), b("Zq"), q(pa, 3), A.max)
+    act(b("h2"), b("val"), AF.Identity, 16448.5)
+    mm(group(q(pc, 0), [(b("E2"), cb("I"))]))
+    act(b("EL"), q(pc, 0), AF.Copy)
+    mm(group(q(pb, 0), [(b("E2"), cb("m127")), (b("del"), cb("m4096")), (b("h2"), cb("I128"))]) +
+       group(q(pb, 1), [(b("E2"), cb("m128")), (b("del"), cb("m4096")), (b("val"), cf("IF")), (b("h2"), cb("nI"))]))
+    ts(b("XA"), q(pb, 0), col(3), A.add)
+    ts(b("XB"), q(pb, 1), col(4), A.add)
+    mm(group(q(pc, 1), [(cb("P2"), b("EL"))]))
+    ts(b("h"), q(pc, 1), col(5), A.is_equal)
+    ts(b("hf"), q(pc, 1), col(5), A.is_equal)
+    mm(group(q(pd, 0), [(cf("TC"), b("hf"))]) + group(q(pd, 1), [(cf("TS"), b("hf"))]) + group(q(pd, 2), [(b("h"), cb("tri"))]))
+    tt(b("PP", 0, 256), b("AB", 0, 256), q(pd, 0, 2), A.mult)
+    mm(group(q(pc, 0), [(b("PP", 0, 128), cf("IV")), (b("PP", 128, 256), cf("IV"))]))
+    act(b("fi"), q(pc, 0), AF.Copy)
+    tt(b("fm"), b("fi"), q(pd, 2), A.mult)
+    route(pb)
+    tt(b("w"), b("fm"), q(pb, 0), A.add)
+    ts(b("pi"), b("w"), 4095, A.bitwise_and)
+    cp(b("pf"), b("pi"))
+    mm(group(q(pa, 0), [(b("pf"), cf("IF"))]))
+    if t < RO:
+        cp(R("po", o, o + 128), q(pa, 0))
+    act(R("ps", o, o + 128), q(pa, 0), AF.Copy)
+    hop(t, h, "e")
+
+
+def build():
+    def load(q, sem, dst, src):
+        op(q, 60, [lambda g, T: g.sync.dma_start(ap(T, dst), T[src][:])], [], [("dma_" + sem, 0, 1, 1)])
+        op("X", 2500, [], [("dma_" + sem, 0, 1, 1)], [dst], sem=sem, inc=16)
+
+    load("Y", "ld0", R("ei", 0, 256), "enz")
+    load("Y", "ld1", R("ct", 0, 4096), "cont")
+    load("Y", "ld2", R("zi", 0, 256), "subs")
+
+    def send(dst_of, src, dst, sem):
+        def f(g, T, core, topo):
+            to = T.cores[(T.rank_of(core) + dst_of) % len(T.cores)]
+            rid, pid, _ = topo.addr(to)
+            m = sum(1 << e for e in topo.engines(core, to)[::2])
+            g.remote_dma(ap(T, dst), ap(T, src), T.sem[sem], T.sem.snt, pid, rid, m)
+            return bin(m).count("1")
+        op("R", 1000, [f], [src], [("net_" + sem, 0, 1, 1)])
+        op("X", NET, [], [("net_" + sem, 0, 1, 1)], [dst], sem=sem, inc=4)
+
+    def hop(t, h, kind):
+        o = 256 * (t - 1) + 128 * h
+        n = o + 256
+        for x in ("o", "s"):
+            if x == "o" and t == RO:
+                continue
+            s = (kind + x if kind == "z" else kind + x) + "%d%d" % (t, h)
+            src = ("e" + x) if kind == "z" else ("p" + x)
+            send(1 if kind == "z" else 2, R(src, o, o + 128), R(kind + x, n, n + 128), s)
+
+    n0 = len(OPS)
+    for h in range(NH):
+        c = R("ei", 128 * h, 128 * h + 128)
+        cp(R("eo", 128 * h, 128 * h + 128), c)
+        cp(R("es", 128 * h, 128 * h + 128), c)
+    for h in range(NH):
+        c = R("zi", 128 * h, 128 * h + 128)
+        cp(R("zo", 128 * h, 128 * h + 128), c)
+        cp(R("zs", 128 * h, 128 * h + 128), c)
+    constants()
+    for t in range(1, RO + 1):
+        for h in range(NH):
+            half_round(t, h, hop)
+    o = 256 * RO
+    for src, dst in (("zs", "ysub"), ("es", "yenz")):
+        for h in range(NH):
+            op("Y", 60, [lambda g, T, src=src, dst=dst, h=h: g.sync.dma_start(T[dst][:, 128 * h:128 * h + 128], T[src][:, o + 128 * h:o + 128 * h + 128])],
+               [R(src, o + 128 * h, o + 128 * h + 128)], [], sem="out", inc=16)
+
+
+def analyse():
+    hist = {}
+    for i, x in enumerate(OPS):
+        deps = {}
+        if x["dep"] is not None:
+            deps[x["dep"]] = True
+        acc = [(r, False) for r in x["r"]] + [(w, True) for w in x["w"]]
+        for (buf, lo, hi, stp), wr in acc:
+            psum = buf in SCRATCH and SCRATCH[buf][0] == "psum"
+            for (l2, h2, s2, w2, j) in hist.get(buf, []):
+                over = lo < h2 and l2 < hi
+                y = OPS[j]
+                if over and stp == s2 and stp > 1 and (lo - l2) % stp != 0:
+                    over = False
+                if psum and y["e"] != x["e"]:
+                    deps[j] = True
+                elif over and w2 and not wr:
+                    deps[j] = True
+                elif over and (wr or w2):
+                    deps[j] = deps.get(j, False) or y["e"] != x["e"] or x["e"] != "P"
+        x["deps"] = deps
+        for (buf, lo, hi, stp), wr in acc:
+            lst = hist.setdefault(buf, [])
+            psum = buf in SCRATCH and SCRATCH[buf][0] == "psum"
+            if wr and stp == 1:
+                lst[:] = [e for e in lst if not (lo <= e[0] and e[1] <= hi and not (psum and OPS[e[4]]["e"] != x["e"] and False)) or e[4] == i]
+            if psum and wr and x["e"] == "P" and lo == 0 and False:
+                lst.clear()
+            lst.append((lo, hi, stp, wr, i))
+            if psum:
+                while len(lst) > 400:
+                    lst.pop(0)
+
+
+def schedule():
+    n = len(OPS)
+    succ = [[] for _ in range(n)]
+    nd = [0] * n
+    for i, x in enumerate(OPS):
+        for j in x["deps"]:
+            succ[j].append(i)
+            nd[i] += 1
+    pri = [0.0] * n
+    for i in range(n - 1, -1, -1):
+        pri[i] = OPS[i]["d"] + max([pri[s] + 60 for s in succ[i]], default=0.0)
+    ready = {}
+    t0 = [0.0] * n
+    for i in range(n):
+        if nd[i] == 0:
+            ready.setdefault(OPS[i]["e"], set()).add(i)
+    free, order, end = {}, [], [0.0] * n
+    while len(order) < n:
+        best = None
+        for e, s in ready.items():
+            for i in s:
+                st = t0[i] if e == "X" else max(free.get(e, 0.0), t0[i])
+                k = (st, -pri[i], i)
+                if best is None or k < best[0]:
+                    best = (k, i, e)
+        (st, _, _), i, e = best
+        ready[e].discard(i)
+        end[i] = st + OPS[i]["d"]
+        if e != "X":
+            free[e] = end[i]
+        order.append(i)
+        for s in succ[i]:
+            lag = 60.0 if OPS[s]["deps"][i] else 0.0
+            t0[s] = max(t0[s], end[i] + lag)
+            nd[s] -= 1
+            if nd[s] == 0:
+                ready.setdefault(OPS[s]["e"], set()).add(s)
+    return order, max(end)
+
+
+PLAN = []
+
+
+def plan():
+    if not PLAN:
+        build()
+        analyse()
+        order, tot = schedule()
+        PLAN.append(order)
+        PLAN.append(tot)
+    return PLAN[0]
+
+
+QS = {"P": "qP", "V": "qV", "S": "qS", "G": "qG"}
+
+
+def rank_program(g, core, T, topo):
+    if T.rank_of(core) is None:
+        return
+    order = plan()
+    queue = {"P": g.tensor, "V": g.vector, "S": g.scalar, "G": g, "R": g, "Y": g.sync}
+    qname = {"G": "g", "R": "g"}
+    cnt, done, know, clock, sent = {}, {}, {}, {}, 0
+    for i in order:
+        x = OPS[i]
+        e = x["e"]
+        if e == "X":
+            done[i] = (x["sem"], x["inc"])
+            clock[i] = {}
+            continue
+        qn = qname.get(e, e)
+        kn = know.setdefault(qn, {})
+        need = {}
+        for j, w in x["deps"].items():
+            if w and done.get(j) is not None:
+                s, v = done[j]
+                if need.get(s, (0, 0))[0] < v:
+                    need[s] = (v, j)
+        for s, (v, j) in sorted(need.items(), key=lambda z: -z[1][1]):
+            if kn.get(s, 0) >= v:
+                continue
+            queue[e].wait_ge(T.sem[s], v)
+            for s2, v2 in clock[j].items():
+                kn[s2] = max(kn.get(s2, 0), v2)
+            kn[s] = max(kn.get(s, 0), v)
+        clock[i] = dict(kn)
+        if e in QS:
+            s = QS[e]
+            for f in x["f"]:
+                f(g, T).then_inc(T.sem[s], 1)
+                cnt[s] = cnt.get(s, 0) + 1
+            done[i] = (s, cnt[s])
+        elif e == "R":
+            for f in x["f"]:
+                sent += f(g, T, core, topo)
+            done[i] = None
+        else:
+            sem = x["sem"]
+            if sem is None:
+                sem = OPS[i]["w"][0][0][4:]
+            for f in x["f"]:
+                f(g, T).then_inc(T.sem[sem], 16)
+                cnt[sem] = cnt.get(sem, 0) + 16
+            done[i] = None
+    for s in list(QS.values()) + ["out", "ld0", "ld1", "ld2"]:
+        if cnt.get(s, 0):
+            g.sync.wait_ge(T.sem[s], cnt[s])
+    g.wait_ge(T.sem.snt, sent)

@@ -3,10 +3,16 @@ from concourse.mybir import AluOpType as A, ActivationFunctionType as AF
 
 RO, LH = 4, 128
 NH = 2
-SC = 1.0
-PC = 0.5
-GC = 1.55
-NET = 4000.0
+FV, FS = 55.0, 65.0
+SC = 0.83
+PC = 0.42
+GC = 1.35
+NET = 3500.0
+LAG = 50.0
+RW, BONUS = 7000.0, {"E2": 8000.0, "psc": -1500.0, "ps": 1500.0, "fi": -8000.0, "po": 1500.0, "val": 1500.0, "hS": 1500.0, "V": 12000.0, "cmp": -1500.0}
+NV = 4
+VCUT = [("S", 32), ("V", 32), ("S", 32), ("S", 32)]
+YCUT = [("S", 32)] * 4
 SCRATCH, SEMAPHORES = {}, []
 
 
@@ -23,7 +29,7 @@ CB = {}
 for _n, _w in ([("I", 128), ("nI", 128), ("I128", 128), ("m127", 128), ("m128", 128), ("m4096", 128), ("m64", 128), ("p32", 128),
                ("R128", 128), ("mR", 128), ("A1", 128), ("A2", 128), ("B1", 128), ("B2", 128), ("P1", 128), ("P2", 128), ("Sp", 128), ("tri", 128),
                ("ones", 128), ("cC", 128), ("cD", 128), ("odd", 256), ("UU", 128), ("zero", 128), ("neg", 128), ("pos", 128), ("keep", 128),
-               ("b16", 16), ("b32", 16), ("bm16", 16)] + [("W%d" % k, 128) for k in range(16)]):
+               ("b16", 16), ("b32", 16), ("bm16", 16), ("b16x", 16)] + [("W%d" % k, 128) for k in range(16)]):
     CB[_n] = (sum(w for _, w in CB.values()), _w)
 _sb("cb", sum(w for _, w in CB.values()))
 CF = {}
@@ -40,7 +46,7 @@ for _n, _w, _d in (("KI", 128, F32), ("KD", 128, F32), ("KV", 128, F32), ("KT", 
 for _h in range(NH):
     for _n, _w, _d in (("V", 2048, BF), ("Y", 2048, BF), ("cmp", 2048, BF), ("mx", 2048, BF), ("PA", 2048, F16), ("PB", 2048, F16), ("km", 128, F32),
                        ("r8", 8, F32), ("E", 128, BF), ("q1", 128, BF), ("q2", 128, BF), ("r", 128, F32), ("X", 128, BF), ("Mx", 128, BF),
-                       ("Mn", 128, BF), ("LT", 384, BF), ("r16", 128, BF), ("hS", 128, BF), ("XA", 128, F16), ("XB", 128, F16), ("v", 128, I32),
+                       ("Mn", 128, BF), ("LT", 384, BF), ("r16", 128, BF), ("hS", 128, BF), ("XA", 256, F16), ("XB", 256, F16), ("v", 128, I32),
                        ("S", 128, I32), ("cd", 128, I32), ("q", 128, F32), ("Zq", 128, F32), ("pr", 128, I32), ("F", 128, I32), ("m2", 128, F32),
                        ("val", 128, F32), ("del", 128, BF), ("E2", 128, BF), ("h2", 128, BF), ("EL", 128, BF), ("h", 128, BF), ("hf", 128, F32),
                        ("AB", 256, F32), ("PP", 256, F32), ("fi", 128, F32), ("fm", 128, F32), ("w", 128, I32), ("pi", 128, I32), ("pf", 128, F32)):
@@ -83,7 +89,7 @@ def isp(r):
     return SCRATCH[r[0]][0] == "psum"
 
 
-OPS = []
+OPS, MARK = [], []
 
 
 def op(eng, dur, fns, reads, writes, sem=None, inc=1, dep=None):
@@ -96,7 +102,7 @@ def two(rs):
 
 
 def cyc(n, x):
-    return max(64.0, n * x) * SC + 8.0
+    return n * x * SC + FV
 
 
 def ts(out, a, s1, op0, s2=None, op1=None):
@@ -128,12 +134,15 @@ def scan(out, d0, d1, o0, o1):
               [lambda g, T: g.vector.tensor_tensor_scan(ap(T, out), ap(T, d0), ap(T, d1), 0.0, o0, o1)], [d0, d1], [out])
 
 
-def act(out, a, func, bias=None):
+def act(out, a, func, bias=None, scale=None):
     def f(g, T):
-        if bias is None:
-            return g.scalar.activation(ap(T, out), ap(T, a), func)
-        return g.scalar.activation(ap(T, out), ap(T, a), func, bias=bias)
-    return op("S", ncol(out) * SC + 20, [f], [a], [out])
+        kw = {}
+        if bias is not None:
+            kw["bias"] = bias
+        if scale is not None:
+            kw["scale"] = ap(T, scale) if isinstance(scale, tuple) else scale
+        return g.scalar.activation(ap(T, out), ap(T, a), func, **kw)
+    return op("S", ncol(out) * SC + FS, [f], [a] + ([scale] if isinstance(scale, tuple) else []), [out])
 
 
 def gather(eng, out, offs):
@@ -175,8 +184,11 @@ def constants():
     iota(UM, [[0, 8], [1, 16]], 0, 0)
     iota(pi, [[0, 2]], 0, 1)
     iota(KT, [[16, 8], [1, 16]], 0, -1)
-    for n, c in (("I", 1.0), ("nI", -1.0), ("I128", 1.0 / 128), ("m127", -127.0), ("m128", -128.0), ("m4096", -4096.0), ("m64", -64.0), ("p32", 32.0)):
-        ts(cb(n), KD, 0.0, A.is_equal, c, A.mult)
+    for n, c in (("I", 1.0), ("nI", -1.0), ("I128", 1.0 / 128), ("m127", -127.0), ("m128", -128.0), ("m4096", -4096.0), ("m64", -32.0), ("p32", 16.0)):
+        if n == "I":
+            ts(cb(n), KD, 0.0, A.is_equal)
+        else:
+            act(cb(n), cb("I"), AF.Copy, scale=c)
     fill(cb("ones"), 1.0); fill(cb("zero"), 0.0)
     for h in range(NH):
         fill(R("E%d" % h, 0, 128), 0.0)
@@ -185,9 +197,10 @@ def constants():
     ts(b8, K8, 15.0, A.is_le)
     tt(b8, b8, t8, A.mult)
     for half in (0, 8):
-        ts(cb("b16", half, half + 8), b8, 1.0, A.mult)
-    ts(cb("b32", 0, 8), b8, 32.0, A.mult)
-    ts(cb("bm16", 0, 8), b8, -16.0, A.mult)
+        act(cb("b16", half, half + 8), b8, AF.Copy)
+    act(cb("b32", 0, 8), b8, AF.Copy, scale=32.0)
+    act(cb("bm16", 0, 8), b8, AF.Copy, scale=-16.0)
+    act(cb("b16x", 0, 8), b8, AF.Copy, scale=16.0)
     ts(R("ch", 0, 8), b8, 128.0, A.mult)
     ts(R("ch", 16, 24), b8, 1.0, A.mult)
     ts(GG, KI, 0.0, A.is_ge)
@@ -211,19 +224,20 @@ def constants():
     c0 = CB["odd"][0]
     fill(R("cb", c0, c0 + 128), 0.0)
     ts(R("cb", c0 + 128, c0 + 256), t1, -2.0, A.mult)
-    for w, a1, a2 in ((127.0, "A1", "A2"), (128.0, "B1", "B2"), (1.0, "P1", "P2")):
-        ts(cb(a2), KI, 15.0, A.is_equal, w, A.mult)
-        ts(t2, KD, 0.0, A.is_equal, w, A.mult)
-        tt(cb(a1), t2, cb(a2), A.subtract)
+    ts(cb("P2"), KI, 15.0, A.is_equal)
+    tt(cb("P1"), cb("I"), cb("P2"), A.subtract)
+    for w, a in ((127.0, "A"), (128.0, "B")):
+        for x in "12":
+            act(cb(a + x), cb("P" + x), AF.Copy, scale=w)
     ts(t1, KD, 0.0, A.is_equal, 4096.0, A.mult)
     ts(t2, KD, 1.0, A.is_equal, 4096.0, A.mult)
     tt(t1, t1, t2, A.subtract)
     ts(t2, UM, 1.0, A.is_ge)
     tt(cb("Sp"), t1, t2, A.mult)
-    ts(cb("R128"), KV, 15.0, A.is_equal, 1.0 / 128, A.mult)
-    ts(cb("mR"), KV, 15.0, A.is_equal, -1.0, A.mult)
     ts(cf("RF"), KV, 15.0, A.is_equal)
-    ts(cf("IF"), KD, 0.0, A.is_equal)
+    act(cb("R128"), cf("RF"), AF.Copy, scale=1.0 / 128)
+    act(cb("mR"), cf("RF"), AF.Copy, scale=-1.0)
+    act(cf("IF"), cb("I"), AF.Copy)
     ts(t1, KT, 0.0, A.is_ge)
     tt(cb("tri"), t1, GG, A.mult)
     ts(pi, pi, 15, A.bitwise_and)
@@ -231,7 +245,7 @@ def constants():
     cp(ri, R("k_pi", 0, 1))
     ts(col(1), ri, 1.0, A.is_ge, -4096.0, A.mult)
     ts(col(2), col(1), 960.0 + 16512.0, A.add)
-    ts(col(1), col(1), 127 * 7.5 + 96 - 129, A.add)
+    ts(col(1), col(1), 127 * 7.5 + 96 - 129 - 16, A.add)
     ts(col(3), ri, 127.0, A.mult, -129.0, A.add)
     ts(col(4), ri, 128.0, A.mult, 16512.0, A.add)
     ts(col(5), ri, -1.0, A.mult, 16.0, A.add)
@@ -274,13 +288,14 @@ def constants():
     for j, name in enumerate(("DA", "DB", "TC", "TS", "IV")):
         c = CF[name][0]
         for q in range(8):
-            ts(R("cf", c + 16 * q, c + 16 * q + 16), R("k_a80", 16 * j, 16 * j + 16), R("b8", q, q + 1), A.mult)
+            act(R("cf", c + 16 * q, c + 16 * q + 16), R("k_a80", 16 * j, 16 * j + 16), AF.Copy, scale=R("b8", q, q + 1))
 
 
 M4, M16 = 1.5 * 2 ** 25, 1.5 * 2 ** 27
 
 
 def half_round(t, h, hop):
+    MARK.append((len(OPS), 2 * t + h))
     b = lambda n, lo=0, hi=128: R("%s%d" % (n, h), lo, hi)
     pa, pb, pc, pd = ["ps%s%d" % (x, h) for x in "abcd"]
     q = lambda p, j, k=1: R(p, 128 * j, 128 * (j + k))
@@ -288,36 +303,49 @@ def half_round(t, h, hop):
     eo, es, zo, zs = R("eo", o, o + 128), R("es", o, o + 128), R("zo", o, o + 128), R("zs", o, o + 128)
     col = lambda j: R("col", j, j + 1)
     hop(t, h, "z")
-    gather("S", b("V", 0, 2048), eo)
-    gather("S", b("Y", 0, 2048), zo)
+    for buf, ls, cuts in (("V", (eo[0], eo[1]), VCUT), ("Y", (zo[0], zo[1]), YCUT)):
+        c = 0
+        for eng, w in cuts:
+            gather(eng, b(buf, 16 * c, 16 * (c + w)), R(ls[0], ls[1] + c, ls[1] + c + w))
+            c += w
     act(b("hS"), es, AF.Identity, 16448.5)
-    mm([(q(pd, 0), cb("I"), R("V%d" % h, 15, 2048, 16), True, True)])
-    for p in range(16):
-        tt(b("mx", 128 * p, 128 * p + 128), R("Y%d" % h, p, 2048, 16), q(pd, 0), A.max)
+    v15 = R("V%d" % h, 15, 2048, 16)
+    for c in range(0, 16 - NV, 4):
+        for j in range(4):
+            mm(group(q(pd, j), [(cb("I"), R("Y%d" % h, c + j, 2048, 16)), (cb("nI"), v15)]))
+        act(b("mx", 128 * c, 128 * c + 512), q(pd, 0, 4), AF.Abs)
+    if NV:
+        mm([(q(pc, 0), cb("I"), v15, True, True)])
+        for p in range(16 - NV, 16):
+            tt(b("mx", 128 * p, 128 * p + 128), R("Y%d" % h, p, 2048, 16), q(pc, 0), A.max)
     mm([(q(pd, 1), cb("ones"), cb("cD"), True, False)])
     for p in range(16):
-        dst = R(pd, 128 + p, 256, 16)
-        mm([(dst, b("mx", 128 * p, 128 * p + 128), cb("b32", 0, 8), False, False),
-            (dst, R("Y%d" % h, p, 2048, 16), cb("bm16", 0, 8), False, p == 15)])
+        dst, x = R(pd, 128 + p, 256, 16), b("mx", 128 * p, 128 * p + 128)
+        if p < 16 - NV:
+            mm([(dst, x, cb("b16x", 0, 8), False, p == 15)])
+        else:
+            mm([(dst, x, cb("b32", 0, 8), False, False), (dst, R("Y%d" % h, p, 2048, 16), cb("bm16", 0, 8), False, False),
+                (dst, v15, cb("bm16", 0, 8), False, p == 15)])
     scan(b("km"), cb("pos"), q(pd, 1), A.add, A.min)
     km = R("km%d" % h, 15, 128, 16)
     ts(b("r8", 0, 8), km, M16, A.add, M16, A.subtract)
     tt(R("E%d" % h, 15, 128, 16), km, b("r8", 0, 8), A.subtract)
     for c in range(4):
         bank = pa if c % 2 == 0 else pb
-        lst = []
         for j in range(4):
             k = 4 * c + j
-            lst += group(q(bank, j), [(cb("I"), R("V%d" % h, k, 2048, 16)), (cb("nI"), R("V%d" % h, (k + 1) % 16, 2048, 16))])
-        mm(lst)
+            mm(group(q(bank, j), [(cb("I"), R("V%d" % h, k, 2048, 16)), (cb("nI"), R("V%d" % h, (k + 1) % 16, 2048, 16))]))
         act(b("cmp", 512 * c, 512 * c + 512), q(bank, 0, 4), AF.Sign, -0.5)
-    mm(group(q(pc, 0), [(cb("ones"), cb("cC"))] + [(b("cmp", 128 * k, 128 * k + 128), cb("W%d" % k)) for k in range(16)]))
-    mm([(q(pc, 1, 2), cb("zero") if t == 1 else b("h"), cb("odd"), True, False)] +
-       [(R(pc, 128 + 15 - k, 384, 16), b("cmp", 128 * k, 128 * k + 128), cb("b16"), False, k == 15) for k in range(16)])
+    mm([(q(pc, 0), cb("ones"), cb("cC"), True, False)])
+    mm([(q(pa, 0, 2), cb("zero") if t == 1 else b("h"), cb("W0", 0, 256) if t == 1 else cb("odd"), True, False)])
+    for k in range(0, 16, 2):
+        mm([(q(pc, 0), b("cmp", 128 * j, 128 * j + 128), cb("W%d" % j), False, j == 15) for j in (k, k + 1)])
+    for k in range(0, 16, 4):
+        mm([(R(pa, 15 - j, 256, 16), b("cmp", 128 * j, 128 * j + 128), cb("b16"), False, j == 15) for j in range(k, k + 4)])
     ts(b("r"), q(pc, 0), M4, A.add, M4, A.subtract)
     scan(b("X"), q(pc, 0), b("r"), A.add, A.subtract)
-    ts(b("q1"), q(pc, 2), -5.0, A.is_gt)
-    ts(b("q2"), q(pc, 1), 3.0, A.is_gt)
+    act(b("q1"), q(pa, 1), AF.Sign, 5.0)
+    act(b("q2"), q(pa, 0), AF.Sign, -3.0)
     scan(b("Mx"), cb("neg"), b("X"), A.add, A.max)
     scan(b("Mn"), cb("pos"), b("X"), A.add, A.min)
     mm(group(q(pa, 0), [(b("Mx"), cb("I")), (b("Mn"), cb("nI"))]) + group(q(pa, 1), [(b("X"), cb("I"))]) + group(q(pa, 2), [(b("E"), cb("I"))]))
@@ -325,19 +353,26 @@ def half_round(t, h, hop):
     sp, X, E = b("LT", 0, 128), b("LT", 128, 256), b("LT", 256, 384)
     mm(group(q(pb, 0), [(cb("P1"), X), (cb("P2"), E)]))
     ts(b("r16"), q(pb, 0), M16, A.add, M16, A.subtract)
-    mm(group(q(pc, 0), [(cb("A1"), X), (cb("A2"), E), (cb("Sp"), sp), (b("q1"), cb("m64")), (b("q2"), cb("p32")), (cb("R128"), b("hS")), (cb("m127"), b("r16"))]) +
-       group(q(pc, 1), [(cb("B1"), X), (cb("B2"), E), (cb("Sp"), sp), (cb("mR"), b("hS")), (cf("RF"), es), (cb("m128"), b("r16"))]))
-    ts(b("XA"), q(pc, 0), col(1), A.add)
-    ts(b("XB"), q(pc, 1), col(2), A.add)
+    XA, XB = q(pc, 0), q(pd, 2)
+    mm([(XA, l, r, i == 0, False) for i, (l, r) in enumerate([(cb("A1"), X), (cb("A2"), E), (cb("Sp"), sp), (b("q1"), cb("m64")), (b("q2"), cb("p32")),
+                                                               (cb("R128"), b("hS"))])])
+    mm([(XB, l, r, i == 0, False) for i, (l, r) in enumerate([(cf("RF"), es), (cb("mR"), b("hS")), (cb("B1"), X), (cb("B2"), E), (cb("Sp"), sp)])])
+    mm([(XA, cb("m127"), b("r16"), False, True)])
+    mm([(XB, cb("m128"), b("r16"), False, True)])
+    ts(b("XA"), XA, col(1), A.add)
+    ts(b("XB"), XB, col(2), A.add)
     mm(group(q(pc, 2), [(cf("DA"), es)]) + group(q(pc, 3), [(cf("DB"), es)]))
     act(b("AB", 0, 256), q(pc, 2, 2), AF.Copy)
 
     def route(bank):
-        for p in range(16):
-            x, y = b("PA", 128 * p, 128 * p + 128), b("PB", 128 * p, 128 * p + 128)
-            ts(x, b("XA"), 127.0 * p, A.max, 127.0 * (p + 1), A.min)
-            ts(y, b("XB"), 128.0 * p, A.max, 128.0 * (p + 1), A.min)
-            mm(group(R(bank, p, 128, 16), [(x, R("ch", 0, 8)), (y, R("ch", 16, 24))]))
+        ts(b("XA", 128, 256), b("XA"), -8 * 127.0, A.add)
+        ts(b("XB", 128, 256), b("XB"), -8 * 128.0, A.add)
+        for p in range(8):
+            ts(b("PA", 256 * p, 256 * p + 256), b("XA", 0, 256), 127.0 * p, A.max, 127.0 * (p + 1), A.min)
+            ts(b("PB", 256 * p, 256 * p + 256), b("XB", 0, 256), 128.0 * p, A.max, 128.0 * (p + 1), A.min)
+            for k in (0, 1):
+                c = 256 * p + 128 * k
+                mm(group(R(bank, p + 8 * k, 128, 16), [(b("PA", c, c + 128), R("ch", 0, 8)), (b("PB", c, c + 128), R("ch", 16, 24))]))
 
     mm(group(q(pa, 0), [(zs, cf("IF"))]))
     route(pd)
@@ -356,15 +391,19 @@ def half_round(t, h, hop):
     tt(q(pa, 3), b("S"), q(pa, 2), A.add)
     tt(b("val"), b("Zq"), q(pa, 3), A.max)
     act(b("h2"), b("val"), AF.Identity, 16448.5)
-    mm(group(q(pc, 0), [(b("E2"), cb("I"))]))
-    act(b("EL"), q(pc, 0), AF.Copy)
-    mm(group(q(pb, 0), [(b("E2"), cb("m127")), (b("del"), cb("m4096")), (b("h2"), cb("I128"))]) +
-       group(q(pb, 1), [(b("E2"), cb("m128")), (b("del"), cb("m4096")), (b("val"), cf("IF")), (b("h2"), cb("nI"))]))
-    ts(b("XA"), q(pb, 0), col(3), A.add)
-    ts(b("XB"), q(pb, 1), col(4), A.add)
-    mm(group(q(pc, 1), [(cb("P2"), b("EL"))]))
-    ts(b("h"), q(pc, 1), col(5), A.is_equal)
-    ts(b("hf"), q(pc, 1), col(5), A.is_equal)
+    XA, XB = q(pb, 0), q(pc, 2)
+    mm([(XA, b("E2"), cb("m127"), True, False), (XA, b("del"), cb("m4096"), False, False)])
+    mm([(XB, b("E2"), cb("m128"), True, False), (XB, b("del"), cb("m4096"), False, False)])
+    mm(group(q(pd, 3), [(b("E2"), cb("I"))]))
+    act(b("EL"), q(pd, 3), AF.Copy)
+    mm(group(q(pd, 2), [(cb("P2"), b("EL"))]))
+    ts(b("hf"), q(pd, 2), col(5), A.is_equal)
+    act(b("h"), b("hf"), AF.Copy)
+    mm([(XB, b("val"), cf("IF"), False, False)])
+    mm([(XA, b("h2"), cb("I128"), False, True)])
+    mm([(XB, b("h2"), cb("nI"), False, True)])
+    ts(b("XA"), XA, col(3), A.add)
+    ts(b("XB"), XB, col(4), A.add)
     mm(group(q(pd, 0), [(cf("TC"), b("hf"))]) + group(q(pd, 1), [(cf("TS"), b("hf"))]) + group(q(pd, 2), [(b("h"), cb("tri"))]))
     tt(b("PP", 0, 256), b("AB", 0, 256), q(pd, 0, 2), A.mult)
     mm(group(q(pc, 0), [(b("PP", 0, 128), cf("IV")), (b("PP", 128, 256), cf("IV"))]))
@@ -394,11 +433,11 @@ def build():
         def f(g, T, core, topo):
             to = T.cores[(T.rank_of(core) + dst_of) % len(T.cores)]
             rid, pid, _ = topo.addr(to)
-            m = sum(1 << e for e in topo.engines(core, to)[::2])
+            m = sum(1 << e for e in topo.engines(core, to))
             g.remote_dma(ap(T, dst), ap(T, src), T.sem[sem], T.sem.snt, pid, rid, m)
             return bin(m).count("1")
         op("R", 1000, [f], [src], [("net_" + sem, 0, 1, 1)])
-        op("X", NET, [], [("net_" + sem, 0, 1, 1)], [dst], sem=sem, inc=4)
+        op("X", NET, [], [("net_" + sem, 0, 1, 1)], [dst], sem=sem, inc=8)
 
     def hop(t, h, kind):
         o = 256 * (t - 1) + 128 * h
@@ -446,6 +485,8 @@ def analyse():
                     over = False
                 if psum and y["e"] != x["e"]:
                     deps[j] = True
+                elif psum and x["e"] == "P":
+                    deps[j] = deps.get(j, False)
                 elif over and w2 and not wr:
                     deps[j] = True
                 elif over and (wr or w2):
@@ -464,29 +505,33 @@ def analyse():
                     lst.pop(0)
 
 
-def schedule():
+def schedule(rw=RW, bonus=BONUS):
     n = len(OPS)
-    succ = [[] for _ in range(n)]
-    nd = [0] * n
+    rk = [0] * n
+    for (a, k), (z, _) in zip(MARK, MARK[1:] + [(n, 0)]):
+        for i in range(a, z):
+            rk[i] = k
+    succ, nd = [[] for _ in range(n)], [0] * n
     for i, x in enumerate(OPS):
+        nd[i] = len(x["deps"])
         for j in x["deps"]:
             succ[j].append(i)
-            nd[i] += 1
-    pri = [0.0] * n
+    path = [0.0] * n
     for i in range(n - 1, -1, -1):
-        pri[i] = OPS[i]["d"] + max([pri[s] + 60 for s in succ[i]], default=0.0)
-    ready = {}
-    t0 = [0.0] * n
+        path[i] = OPS[i]["d"] + max([path[s] + LAG for s in succ[i]], default=0.0)
+        if rk[i] == 0:
+            rk[i] = min([rk[s] for s in succ[i]], default=99)
+    pri = [path[i] - rw * rk[i] + bonus.get(OPS[i]["w"][0][0][:-1] if OPS[i]["w"] else "", 0.0) for i in range(n)]
+    ready, t0, free, order, end = {}, [0.0] * n, {}, [], [0.0] * n
     for i in range(n):
         if nd[i] == 0:
             ready.setdefault(OPS[i]["e"], set()).add(i)
-    free, order, end = {}, [], [0.0] * n
     while len(order) < n:
         best = None
         for e, s in ready.items():
+            f = 0.0 if e == "X" else free.get(e, 0.0)
             for i in s:
-                st = t0[i] if e == "X" else max(free.get(e, 0.0), t0[i])
-                k = (st, -pri[i], i)
+                k = (max(f, t0[i]), -pri[i], i)
                 if best is None or k < best[0]:
                     best = (k, i, e)
         (st, _, _), i, e = best
@@ -496,8 +541,7 @@ def schedule():
             free[e] = end[i]
         order.append(i)
         for s in succ[i]:
-            lag = 60.0 if OPS[s]["deps"][i] else 0.0
-            t0[s] = max(t0[s], end[i] + lag)
+            t0[s] = max(t0[s], end[i] + (LAG if OPS[s]["deps"][i] else 0.0))
             nd[s] -= 1
             if nd[s] == 0:
                 ready.setdefault(OPS[s]["e"], set()).add(s)

@@ -3,14 +3,15 @@ from concourse.mybir import AluOpType as A, ActivationFunctionType as AF
 
 RO, LH = 4, 128
 NH = 2
-FV, FS = 55.0, 65.0
+FV, FS = 20.0, 30.0
 SC = 0.83
-PC = 0.42
+PC = 0.5
 GC = 1.35
-NET = 3500.0
-LAG = 50.0
-RW, BONUS = 7000.0, {"E2": 8000.0, "psc": -1500.0, "ps": 1500.0, "fi": -8000.0, "po": 1500.0, "val": 1500.0, "hS": 1500.0, "V": 12000.0, "cmp": -1500.0}
-NV = 4
+NET = 4500.0
+LAG = 150.0
+RW, BONUS = 10500.0, {"XB": 1500.0, "AB": -5000.0, "po": -8000.0, "h": 1500.0, "km": 5000.0, "fi": -8000.0, "E2": 5000.0, "d": 5000.0, "X": 12000.0,
+                      "q1": 5000.0, "F": 3000.0, "ps": -1500.0, "S": 1500.0, "PP": 3000.0, "pr": 3000.0, "Y": -1500.0, "hS": -1500.0}
+NV = 12
 VCUT = [("S", 32), ("V", 32), ("S", 32), ("S", 32)]
 YCUT = [("S", 32)] * 4
 SCRATCH, SEMAPHORES = {}, []
@@ -23,33 +24,36 @@ def _sb(name, cols, dtype="bfloat16"):
 F32, BF, I32, U16, F16 = "float32", "bfloat16", "int32", "uint16", "float16"
 _sb("ct", 4096)
 _sb("ei", 256, I32); _sb("zi", 256, I32)
-_sb("eo", 1280, U16); _sb("es", 1280, F32); _sb("zo", 1280, U16); _sb("zs", 1280, F32)
-_sb("po", 1024, U16); _sb("ps", 1024, F32)
+_sb("eo", 1280, U16); _sb("es", 1280, F16); _sb("zo", 1280, U16); _sb("zs", 1280, F16)
+_sb("po", 1024, U16); _sb("ps", 768, F16)
+_sb("pz", 256, F32); _sb("ef", 256, F32); _sb("yz", 256, F32)
 CB = {}
-for _n, _w in ([("I", 128), ("nI", 128), ("I128", 128), ("m127", 128), ("m128", 128), ("m4096", 128), ("m64", 128), ("p32", 128),
-               ("R128", 128), ("mR", 128), ("A1", 128), ("A2", 128), ("B1", 128), ("B2", 128), ("P1", 128), ("P2", 128), ("Sp", 128), ("tri", 128),
-               ("ones", 128), ("cC", 128), ("cD", 128), ("odd", 256), ("UU", 128), ("zero", 128), ("neg", 128), ("pos", 128), ("keep", 128),
-               ("b16", 16), ("b32", 16), ("bm16", 16), ("b16x", 16)] + [("W%d" % k, 128) for k in range(16)]):
+for _n, _w in [("I", 128), ("nI", 128), ("I128", 128), ("p127", 128), ("p128", 128), ("m127", 128), ("m128", 128), ("m4096", 128), ("m64", 128),
+               ("p32", 128), ("P2", 128), ("Sp", 128), ("ones", 128), ("c16", 128), ("cD", 128), ("cC", 256), ("neg", 128), ("pos", 128),
+               ("keep", 128), ("b16", 16), ("b16x", 16)]:
     CB[_n] = (sum(w for _, w in CB.values()), _w)
 _sb("cb", sum(w for _, w in CB.values()))
 CF = {}
-for _n in ("IF", "RF", "DA", "DB", "TC", "TS", "IV"):
+for _n in ("DA", "DB", "TC", "TS", "IV", "IF"):
     CF[_n] = (128 * len(CF), 128)
 _sb("cf", 128 * len(CF), F32)
-_sb("ch", 32, F16)
+CH = {}
+for _n, _w in [("b128", 16), ("b1", 16), ("I", 128), ("tri", 128), ("odd", 128)] + [(_x + _y, 128) for _y in "hl" for _x in ("DA", "DB", "TC", "TS")]:
+    CH[_n] = (sum(w for _, w in CH.values()), _w)
+_sb("ch", sum(w for _, w in CH.values()), F16)
 _sb("b8", 8, F32)
 _sb("col", 16, F32)
-for _n, _w, _d in (("KI", 128, F32), ("KD", 128, F32), ("KV", 128, F32), ("KT", 128, F32), ("UM", 128, F32), ("GG", 128, F32), ("t1", 128, F32),
+for _n, _w, _d in (("KI", 128, F32), ("KD", 128, F32), ("KT", 128, F32), ("UM", 128, F32), ("GG", 128, F32), ("t1", 128, F32),
                    ("t2", 128, F32), ("ki", 128, I32), ("pi", 2, I32), ("K8", 8, F32), ("u16f", 16, F32), ("f16", 16, F32), ("im16", 16, F32),
                    ("n80", 80, F32), ("n80i", 80, I32), ("w80", 80, F32), ("x80", 80, F32), ("a80", 80, F32)):
     _sb("k_" + _n, _w, _d)
 for _h in range(NH):
     for _n, _w, _d in (("V", 2048, BF), ("Y", 2048, BF), ("cmp", 2048, BF), ("mx", 2048, BF), ("PA", 2048, F16), ("PB", 2048, F16), ("km", 128, F32),
-                       ("r8", 8, F32), ("E", 128, BF), ("q1", 128, BF), ("q2", 128, BF), ("r", 128, F32), ("X", 128, BF), ("Mx", 128, BF),
-                       ("Mn", 128, BF), ("LT", 384, BF), ("r16", 128, BF), ("hS", 128, BF), ("XA", 256, F16), ("XB", 256, F16), ("v", 128, I32),
+                       ("r8", 8, F32), ("d", 128, BF), ("q1", 128, BF), ("q2", 128, BF), ("r", 128, F32), ("X", 128, BF), ("Mx", 128, BF),
+                       ("Mn", 128, BF), ("LT", 128, BF), ("r16", 128, BF), ("hS", 128, BF), ("XA", 256, F16), ("XB", 256, F16), ("v", 128, I32),
                        ("S", 128, I32), ("cd", 128, I32), ("q", 128, F32), ("Zq", 128, F32), ("pr", 128, I32), ("F", 128, I32), ("m2", 128, F32),
-                       ("val", 128, F32), ("del", 128, BF), ("E2", 128, BF), ("h2", 128, BF), ("EL", 128, BF), ("h", 128, BF), ("hf", 128, F32),
-                       ("AB", 256, F32), ("PP", 256, F32), ("fi", 128, F32), ("fm", 128, F32), ("w", 128, I32), ("pi", 128, I32), ("pf", 128, F32)):
+                       ("val", 128, F32), ("del", 128, BF), ("E2", 128, BF), ("h2", 128, BF), ("EL", 128, BF), ("h", 128, F16),
+                       ("AB", 256, F32), ("PP", 256, F32), ("fi", 128, F32), ("fm", 128, F32), ("w", 128, I32), ("pi", 128, I32), ("pf", 128, F16)):
         _sb("%s%d" % (_n, _h), _w, _d)
     for _n in "abcd":
         SCRATCH["ps%s%d" % (_n, _h)] = ("psum", [128, 512], F32)
@@ -73,12 +77,19 @@ def cf(n):
     return R("cf", c, c + w)
 
 
+def ch(n, w=None):
+    return R("ch", CH[n][0], CH[n][0] + (w or CH[n][1]))
+
+
 def ap(T, r):
+    if r[3] == -1:
+        return T[r[0]][:, r[2] - 1:r[1] - 1:-1] if r[1] else T[r[0]][:, r[2] - 1::-1]
     return T[r[0]][:, r[1]:r[2]:r[3]] if r[3] != 1 else T[r[0]][:, r[1]:r[2]]
 
 
 def ncol(r):
-    return (r[2] - r[1] + r[3] - 1) // r[3]
+    s = abs(r[3])
+    return (r[2] - r[1] + s - 1) // s
 
 
 def dts(r):
@@ -174,77 +185,58 @@ def iota(out, pattern, base, cm):
 
 def constants():
     K = lambda n, w: R("k_" + n, 0, w)
-    KI, KD, KV, KT, UM, GG, t1, t2 = [K(n, 128) for n in ("KI", "KD", "KV", "KT", "UM", "GG", "t1", "t2")]
+    KI, KD, KT, UM, GG, t1, t2 = [K(n, 128) for n in ("KI", "KD", "KT", "UM", "GG", "t1", "t2")]
     ki, pi, K8 = K("ki", 128), K("pi", 2), K("K8", 8)
     col = lambda j: R("col", j, j + 1)
     iota(KI, [[-16, 8], [0, 16]], 0, 1)
     iota(KD, [[1, 128]], 0, -1)
     iota(K8, [[-16, 8]], 0, 1)
-    iota(KV, [[-16, 8], [1, 16]], 0, 1)
     iota(UM, [[0, 8], [1, 16]], 0, 0)
     iota(pi, [[0, 2]], 0, 1)
     iota(KT, [[16, 8], [1, 16]], 0, -1)
-    for n, c in (("I", 1.0), ("nI", -1.0), ("I128", 1.0 / 128), ("m127", -127.0), ("m128", -128.0), ("m4096", -4096.0), ("m64", -32.0), ("p32", 16.0)):
+    for n, c in (("I", 1.0), ("nI", -1.0), ("I128", 1.0 / 128), ("p127", 127.0), ("p128", 128.0), ("m127", -127.0), ("m128", -128.0), ("m4096", -4096.0), ("m64", -32.0), ("p32", 16.0)):
         if n == "I":
             ts(cb(n), KD, 0.0, A.is_equal)
         else:
             act(cb(n), cb("I"), AF.Copy, scale=c)
-    fill(cb("ones"), 1.0); fill(cb("zero"), 0.0)
-    for h in range(NH):
-        fill(R("E%d" % h, 0, 128), 0.0)
+    fill(cb("ones"), 1.0); fill(cb("c16"), 16.0); fill(cb("cC"), 0.0)
+    ts(R("cb", CB["cC"][0], CB["cC"][0] + 128), UM, 0.0, A.is_equal, -1.0 / 128, A.mult)
     b8, t8 = R("b8", 0, 8), R("k_t1", 0, 8)
     ts(t8, K8, 0.0, A.is_ge)
     ts(b8, K8, 15.0, A.is_le)
     tt(b8, b8, t8, A.mult)
     for half in (0, 8):
         act(cb("b16", half, half + 8), b8, AF.Copy)
-    act(cb("b32", 0, 8), b8, AF.Copy, scale=32.0)
-    act(cb("bm16", 0, 8), b8, AF.Copy, scale=-16.0)
     act(cb("b16x", 0, 8), b8, AF.Copy, scale=16.0)
-    ts(R("ch", 0, 8), b8, 128.0, A.mult)
-    ts(R("ch", 16, 24), b8, 1.0, A.mult)
+    ts(ch("b128", 8), b8, 128.0, A.mult)
+    ts(ch("b1", 8), b8, 1.0, A.mult)
+    cp(ch("I"), cb("I"))
     ts(GG, KI, 0.0, A.is_ge)
     ts(t1, KI, 15.0, A.is_le)
     tt(GG, GG, t1, A.mult)
     ts(t1, UM, 7.5, A.subtract, 1.0 / 128, A.mult)
     cp(cb("cD"), t1)
-    ts(cb("cC"), UM, 1.0, A.is_ge, -1.0 / 128, A.mult)
     ts(cb("neg"), UM, 0.0, A.is_equal, -1000.0, A.mult)
     ts(cb("pos"), UM, 0.0, A.is_equal, 1048576.0, A.mult)
     ts(cb("keep"), UM, 1.0, A.is_ge)
-    ts(t1, UM, 1.0, A.is_ge)
-    tt(t1, t1, GG, A.mult)
-    ts(t1, t1, -99.0, A.mult, 99.0, A.add)
-    tt(cb("UU"), t1, UM, A.add)
-    for k in range(16):
-        ts(cb("W%d" % k), cb("UU"), 16.5 - k, A.is_le)
     cp(ki, KI)
     ts(ki, ki, 1, A.bitwise_and)
     tt(t1, ki, GG, A.mult)
-    c0 = CB["odd"][0]
-    fill(R("cb", c0, c0 + 128), 0.0)
-    ts(R("cb", c0 + 128, c0 + 256), t1, -2.0, A.mult)
+    ts(ch("odd"), t1, -2.0, A.mult)
     ts(cb("P2"), KI, 15.0, A.is_equal)
-    tt(cb("P1"), cb("I"), cb("P2"), A.subtract)
-    for w, a in ((127.0, "A"), (128.0, "B")):
-        for x in "12":
-            act(cb(a + x), cb("P" + x), AF.Copy, scale=w)
     ts(t1, KD, 0.0, A.is_equal, 4096.0, A.mult)
-    ts(t2, KD, 1.0, A.is_equal, 4096.0, A.mult)
+    ts(t2, KD, -1.0, A.is_equal, 4096.0, A.mult)
     tt(t1, t1, t2, A.subtract)
-    ts(t2, UM, 1.0, A.is_ge)
+    ts(t2, UM, 14.0, A.is_le)
     tt(cb("Sp"), t1, t2, A.mult)
-    ts(cf("RF"), KV, 15.0, A.is_equal)
-    act(cb("R128"), cf("RF"), AF.Copy, scale=1.0 / 128)
-    act(cb("mR"), cf("RF"), AF.Copy, scale=-1.0)
     act(cf("IF"), cb("I"), AF.Copy)
     ts(t1, KT, 0.0, A.is_ge)
-    tt(cb("tri"), t1, GG, A.mult)
+    tt(ch("tri"), t1, GG, A.mult)
     ts(pi, pi, 15, A.bitwise_and)
     ri = col(0)
     cp(ri, R("k_pi", 0, 1))
-    ts(col(1), ri, 1.0, A.is_ge, -4096.0, A.mult)
-    ts(col(2), col(1), 960.0 + 16512.0, A.add)
+    ts(col(1), ri, 14.0, A.is_le, -4096.0, A.mult)
+    ts(col(2), col(1), 960.0 + 16512.0 + 2048.0, A.add)
     ts(col(1), col(1), 127 * 7.5 + 96 - 129 - 16, A.add)
     ts(col(3), ri, 127.0, A.mult, -129.0, A.add)
     ts(col(4), ri, 128.0, A.mult, 16512.0, A.add)
@@ -289,6 +281,9 @@ def constants():
         c = CF[name][0]
         for q in range(8):
             act(R("cf", c + 16 * q, c + 16 * q + 16), R("k_a80", 16 * j, 16 * j + 16), AF.Copy, scale=R("b8", q, q + 1))
+    hi, lo = R("ch", CH["DAh"][0], CH["DAh"][0] + 512), R("ch", CH["DAl"][0], CH["DAl"][0] + 512)
+    cp(hi, R("cf", 0, 512))
+    tt(lo, R("cf", 0, 512), hi, A.subtract)
 
 
 M4, M16 = 1.5 * 2 ** 25, 1.5 * 2 ** 27
@@ -308,7 +303,7 @@ def half_round(t, h, hop):
         for eng, w in cuts:
             gather(eng, b(buf, 16 * c, 16 * (c + w)), R(ls[0], ls[1] + c, ls[1] + c + w))
             c += w
-    act(b("hS"), es, AF.Identity, 16448.5)
+    ts(b("hS"), es, 2048 + 16448.5, A.add)
     v15 = R("V%d" % h, 15, 2048, 16)
     for c in range(0, 16 - NV, 4):
         for j in range(4):
@@ -317,79 +312,80 @@ def half_round(t, h, hop):
     if NV:
         mm([(q(pc, 0), cb("I"), v15, True, True)])
         for p in range(16 - NV, 16):
-            tt(b("mx", 128 * p, 128 * p + 128), R("Y%d" % h, p, 2048, 16), q(pc, 0), A.max)
+            tt(b("mx", 128 * p, 128 * p + 128), R("Y%d" % h, p, 2048, 16), q(pc, 0), A.subtract)
+        for p in range(16 - NV, 16, 4):
+            x = b("mx", 128 * p, 128 * min(16, p + 4))
+            act(x, x, AF.Abs)
     mm([(q(pd, 1), cb("ones"), cb("cD"), True, False)])
     for p in range(16):
-        dst, x = R(pd, 128 + p, 256, 16), b("mx", 128 * p, 128 * p + 128)
-        if p < 16 - NV:
-            mm([(dst, x, cb("b16x", 0, 8), False, p == 15)])
-        else:
-            mm([(dst, x, cb("b32", 0, 8), False, False), (dst, R("Y%d" % h, p, 2048, 16), cb("bm16", 0, 8), False, False),
-                (dst, v15, cb("bm16", 0, 8), False, p == 15)])
+        mm([(R(pd, 128 + p, 256, 16), b("mx", 128 * p, 128 * p + 128), cb("b16x", 0, 8), False, p == 15)])
     scan(b("km"), cb("pos"), q(pd, 1), A.add, A.min)
     km = R("km%d" % h, 15, 128, 16)
     ts(b("r8", 0, 8), km, M16, A.add, M16, A.subtract)
-    tt(R("E%d" % h, 15, 128, 16), km, b("r8", 0, 8), A.subtract)
     for c in range(4):
         bank = pa if c % 2 == 0 else pb
         for j in range(4):
             k = 4 * c + j
             mm(group(q(bank, j), [(cb("I"), R("V%d" % h, k, 2048, 16)), (cb("nI"), R("V%d" % h, (k + 1) % 16, 2048, 16))]))
         act(b("cmp", 512 * c, 512 * c + 512), q(bank, 0, 4), AF.Sign, -0.5)
-    mm([(q(pc, 0), cb("ones"), cb("cC"), True, False)])
-    mm([(q(pa, 0, 2), cb("zero") if t == 1 else b("h"), cb("W0", 0, 256) if t == 1 else cb("odd"), True, False)])
-    for k in range(0, 16, 2):
-        mm([(q(pc, 0), b("cmp", 128 * j, 128 * j + 128), cb("W%d" % j), False, j == 15) for j in (k, k + 1)])
+    mm([(q(pa, 0, 2), cb("ones"), cb("cC"), True, False)] + ([(q(pa, 1), b("h"), ch("odd"), False, False)] if t > 1 else []))
     for k in range(0, 16, 4):
-        mm([(R(pa, 15 - j, 256, 16), b("cmp", 128 * j, 128 * j + 128), cb("b16"), False, j == 15) for j in range(k, k + 4)])
-    ts(b("r"), q(pc, 0), M4, A.add, M4, A.subtract)
-    scan(b("X"), q(pc, 0), b("r"), A.add, A.subtract)
+        mm([(R(pa, j, 256, 16), b("cmp", 128 * j, 128 * j + 128), cb("b16"), False, j == 15) for j in range(k, k + 4)])
     act(b("q1"), q(pa, 1), AF.Sign, 5.0)
-    act(b("q2"), q(pa, 0), AF.Sign, -3.0)
-    scan(b("Mx"), cb("neg"), b("X"), A.add, A.max)
-    scan(b("Mn"), cb("pos"), b("X"), A.add, A.min)
-    mm(group(q(pa, 0), [(b("Mx"), cb("I")), (b("Mn"), cb("nI"))]) + group(q(pa, 1), [(b("X"), cb("I"))]) + group(q(pa, 2), [(b("E"), cb("I"))]))
-    act(b("LT", 0, 384), q(pa, 0, 3), AF.Copy)
-    sp, X, E = b("LT", 0, 128), b("LT", 128, 256), b("LT", 256, 384)
-    mm(group(q(pb, 0), [(cb("P1"), X), (cb("P2"), E)]))
-    ts(b("r16"), q(pb, 0), M16, A.add, M16, A.subtract)
-    XA, XB = q(pc, 0), q(pd, 2)
-    mm([(XA, l, r, i == 0, False) for i, (l, r) in enumerate([(cb("A1"), X), (cb("A2"), E), (cb("Sp"), sp), (b("q1"), cb("m64")), (b("q2"), cb("p32")),
-                                                               (cb("R128"), b("hS"))])])
-    mm([(XB, l, r, i == 0, False) for i, (l, r) in enumerate([(cf("RF"), es), (cb("mR"), b("hS")), (cb("B1"), X), (cb("B2"), E), (cb("Sp"), sp)])])
-    mm([(XA, cb("m127"), b("r16"), False, True)])
-    mm([(XB, cb("m128"), b("r16"), False, True)])
-    ts(b("XA"), XA, col(1), A.add)
-    ts(b("XB"), XB, col(2), A.add)
-    mm(group(q(pc, 2), [(cf("DA"), es)]) + group(q(pc, 3), [(cf("DB"), es)]))
-    act(b("AB", 0, 256), q(pc, 2, 2), AF.Copy)
+    act(b("q2"), q(pa, 0), AF.Sign, -2.5)
+    scan(q(pc, 0), cb("keep"), q(pa, 0), A.mult, A.add)
+    ts(b("r"), q(pc, 0), M4, A.add, M4, A.subtract)
+    tt(b("d"), b("r"), q(pc, 0), A.subtract)
+    tt(R("d%d" % h, 0, 128, 16), km, b("r8", 0, 8), A.subtract)
+    scan(b("X"), cb("keep"), b("d"), A.mult, A.add)
+    rev = lambda n: R("%s%d" % (n, h), 0, 128, -1)
+    scan(rev("Mx"), cb("neg"), rev("X"), A.add, A.max)
+    scan(rev("Mn"), cb("pos"), rev("X"), A.add, A.min)
+    ts(b("r16"), b("X"), M16, A.add, M16, A.subtract)
+    mm(group(q(pb, 0), [(b("Mx"), cb("I")), (b("Mn"), cb("nI"))]))
+    act(b("LT"), q(pb, 0), AF.Copy)
+    XA, XB = q(pc, 1), q(pd, 2)
+    mm([(XA, b("q1"), cb("m64"), True, False), (XA, b("q2"), cb("p32"), False, False), (XA, cb("I128"), b("hS"), False, False)])
+    mm([(XB, ch("I"), es, True, False), (XB, cb("nI"), b("hS"), False, False)])
+    mm([(XA, b("X"), cb("p127"), False, False), (XA, b("r16"), cb("m127"), False, False)])
+    mm([(XB, b("X"), cb("p128"), False, False), (XB, b("r16"), cb("m128"), False, False)])
+    mm([(XA, cb("Sp"), b("LT"), False, True)])
+    mm([(XB, cb("Sp"), b("LT"), False, True)])
+
+    def keys(ka, kb, ca, cc):
+        ts(b("XA"), ka, ca, A.add)
+        ts(b("XA", 128, 256), ka, ca, A.add, -8 * 127.0, A.add)
+        ts(b("XB"), kb, cc, A.add)
+        ts(b("XB", 128, 256), kb, cc, A.add, -8 * 128.0, A.add)
 
     def route(bank):
-        ts(b("XA", 128, 256), b("XA"), -8 * 127.0, A.add)
-        ts(b("XB", 128, 256), b("XB"), -8 * 128.0, A.add)
         for p in range(8):
             ts(b("PA", 256 * p, 256 * p + 256), b("XA", 0, 256), 127.0 * p, A.max, 127.0 * (p + 1), A.min)
             ts(b("PB", 256 * p, 256 * p + 256), b("XB", 0, 256), 128.0 * p, A.max, 128.0 * (p + 1), A.min)
             for k in (0, 1):
                 c = 256 * p + 128 * k
-                mm(group(R(bank, p + 8 * k, 128, 16), [(b("PA", c, c + 128), R("ch", 0, 8)), (b("PB", c, c + 128), R("ch", 16, 24))]))
+                mm(group(R(bank, p + 8 * k, 128, 16), [(b("PA", c, c + 128), ch("b128", 8)), (b("PB", c, c + 128), ch("b1", 8))]))
 
-    mm(group(q(pa, 0), [(zs, cf("IF"))]))
+    keys(XA, XB, col(1), col(2))
+    mm(group(q(pc, 2), [(ch("DAh"), es), (ch("DAl"), es)]) + group(q(pc, 3), [(ch("DBh"), es), (ch("DBl"), es)]))
+    act(b("AB", 0, 256), q(pc, 2, 2), AF.Copy)
+    mm(group(q(pa, 0), [(zs, ch("I")), (cb("ones"), cb("c16"))]))
     route(pd)
     cp(b("v"), q(pd, 0))
     ts(b("S"), b("v"), 4095, A.bitwise_and)
     ts(b("cd"), b("v"), 12, A.arith_shift_right, 3, A.bitwise_and)
     tt(b("pr"), b("S"), q(pa, 0), A.mult)
     ts(b("del"), b("cd"), 3.0, A.is_ge)
-    ts(b("q"), b("cd"), 1.0, A.is_ge, -8192.0, A.mult)
     ts(b("F"), b("pr"), 5, A.arith_shift_right, 4095, A.bitwise_and)
-    ts(b("m2"), b("cd"), 2.0, A.is_ge)
+    ts(q(pa, 1), b("cd"), 2.0, A.is_ge)
     scan(b("E2"), cb("keep"), b("del"), A.mult, A.add)
-    tt(b("Zq"), b("q"), q(pa, 0), A.add)
-    ts(q(pa, 1), b("F"), 77.0 * t, A.add)
-    tt(q(pa, 2), b("m2"), q(pa, 1), A.mult)
-    tt(q(pa, 3), b("S"), q(pa, 2), A.add)
-    tt(b("val"), b("Zq"), q(pa, 3), A.max)
+    ts(q(pa, 2), b("cd"), 2.0, A.is_ge, 77.0 * t, A.mult)
+    ts(b("q"), b("cd"), 0.0, A.is_equal)
+    tt(b("m2"), b("S"), q(pa, 2), A.add)
+    tt(q(pa, 3), b("q"), q(pa, 0), A.mult)
+    tt(q(pa, 2), b("m2"), q(pa, 3), A.add)
+    tt(b("Zq"), b("F"), q(pa, 1), A.mult)
+    tt(b("val"), b("Zq"), q(pa, 2), A.add)
     act(b("h2"), b("val"), AF.Identity, 16448.5)
     XA, XB = q(pb, 0), q(pc, 2)
     mm([(XA, b("E2"), cb("m127"), True, False), (XA, b("del"), cb("m4096"), False, False)])
@@ -397,26 +393,27 @@ def half_round(t, h, hop):
     mm(group(q(pd, 3), [(b("E2"), cb("I"))]))
     act(b("EL"), q(pd, 3), AF.Copy)
     mm(group(q(pd, 2), [(cb("P2"), b("EL"))]))
-    ts(b("hf"), q(pd, 2), col(5), A.is_equal)
-    act(b("h"), b("hf"), AF.Copy)
+    ts(b("h"), q(pd, 2), col(5), A.is_equal)
     mm([(XB, b("val"), cf("IF"), False, False)])
     mm([(XA, b("h2"), cb("I128"), False, True)])
     mm([(XB, b("h2"), cb("nI"), False, True)])
-    ts(b("XA"), XA, col(3), A.add)
-    ts(b("XB"), XB, col(4), A.add)
-    mm(group(q(pd, 0), [(cf("TC"), b("hf"))]) + group(q(pd, 1), [(cf("TS"), b("hf"))]) + group(q(pd, 2), [(b("h"), cb("tri"))]))
+    keys(XA, XB, col(3), col(4))
+    mm(group(q(pd, 0), [(ch("TCh"), b("h")), (ch("TCl"), b("h"))]) + group(q(pd, 1), [(ch("TSh"), b("h")), (ch("TSl"), b("h"))]) +
+       group(q(pd, 2), [(b("h"), ch("tri"))]))
     tt(b("PP", 0, 256), b("AB", 0, 256), q(pd, 0, 2), A.mult)
     mm(group(q(pc, 0), [(b("PP", 0, 128), cf("IV")), (b("PP", 128, 256), cf("IV"))]))
-    act(b("fi"), q(pc, 0), AF.Copy)
+    act(b("fi"), q(pc, 0), AF.Copy, 2048.0)
     tt(b("fm"), b("fi"), q(pd, 2), A.mult)
     route(pb)
     tt(b("w"), b("fm"), q(pb, 0), A.add)
     ts(b("pi"), b("w"), 4095, A.bitwise_and)
-    cp(b("pf"), b("pi"))
-    mm(group(q(pa, 0), [(b("pf"), cf("IF"))]))
+    ts(b("pf"), b("pi"), -2048.0, A.add)
+    mm(group(q(pa, 0), [(b("pf"), ch("I"))]))
     if t < RO:
-        cp(R("po", o, o + 128), q(pa, 0))
-    act(R("ps", o, o + 128), q(pa, 0), AF.Copy)
+        ts(R("po", o, o + 128), q(pa, 0), 2048.0, A.add)
+        cp(R("ps", o, o + 128), q(pa, 0))
+    else:
+        act(R("pz", 128 * h, 128 * h + 128), q(pa, 0), AF.Copy, 2048.0)
     hop(t, h, "e")
 
 
@@ -447,26 +444,27 @@ def build():
                 continue
             s = (kind + x if kind == "z" else kind + x) + "%d%d" % (t, h)
             src = ("e" + x) if kind == "z" else ("p" + x)
-            send(1 if kind == "z" else 2, R(src, o, o + 128), R(kind + x, n, n + 128), s)
+            if kind == "e" and t == RO:
+                send(2, R("pz", 128 * h, 128 * h + 128), R("ef", 128 * h, 128 * h + 128), s)
+            else:
+                send(1 if kind == "z" else 2, R(src, o, o + 128), R(kind + x, n, n + 128), s)
 
-    n0 = len(OPS)
-    for h in range(NH):
-        c = R("ei", 128 * h, 128 * h + 128)
-        cp(R("eo", 128 * h, 128 * h + 128), c)
-        cp(R("es", 128 * h, 128 * h + 128), c)
-    for h in range(NH):
-        c = R("zi", 128 * h, 128 * h + 128)
-        cp(R("zo", 128 * h, 128 * h + 128), c)
-        cp(R("zs", 128 * h, 128 * h + 128), c)
+    for k in "ez":
+        for h in range(NH):
+            c = R(k + "i", 128 * h, 128 * h + 128)
+            cp(R(k + "o", 128 * h, 128 * h + 128), c)
+            ts(R(k + "s", 128 * h, 128 * h + 128), c, -2048.0, A.add)
     constants()
     for t in range(1, RO + 1):
         for h in range(NH):
             half_round(t, h, hop)
     o = 256 * RO
-    for src, dst in (("zs", "ysub"), ("es", "yenz")):
+    for h in range(NH):
+        ts(R("yz", 128 * h, 128 * h + 128), R("zs", o + 128 * h, o + 128 * h + 128), 2048.0, A.add)
+    for src, dst in (("yz", "ysub"), ("ef", "yenz")):
         for h in range(NH):
-            op("Y", 60, [lambda g, T, src=src, dst=dst, h=h: g.sync.dma_start(T[dst][:, 128 * h:128 * h + 128], T[src][:, o + 128 * h:o + 128 * h + 128])],
-               [R(src, o + 128 * h, o + 128 * h + 128)], [], sem="out", inc=16)
+            op("Y", 60, [lambda g, T, src=src, dst=dst, h=h: g.sync.dma_start(T[dst][:, 128 * h:128 * h + 128], T[src][:, 128 * h:128 * h + 128])],
+               [R(src, 128 * h, 128 * h + 128)], [], sem="out", inc=16)
 
 
 def analyse():

import math
from concourse.mybir import AluOpType as A, ActivationFunctionType as AF

RO, LH = 4, 128
NH = 2
FV, FS = 20.0, 30.0
SC = 0.83
PC = 0.5
GC = 1.35
NET = 4500.0
LAG = 150.0
RW, BONUS = 10500.0, {"XB": 1500.0, "AB": -5000.0, "po": -8000.0, "h": 1500.0, "km": 5000.0, "fi": -8000.0, "E2": 5000.0, "d": 5000.0, "X": 12000.0,
                      "q1": 5000.0, "F": 3000.0, "ps": -1500.0, "S": 1500.0, "PP": 3000.0, "pr": 3000.0, "Y": -1500.0, "hS": -1500.0}
NV = 12
VCUT = [("S", 32), ("V", 32), ("S", 32), ("S", 32)]
YCUT = [("S", 32)] * 4
SCRATCH, SEMAPHORES = {}, []


def _sb(name, cols, dtype="bfloat16"):
    SCRATCH[name] = ("sbuf", [128, cols], dtype)


F32, BF, I32, U16, F16 = "float32", "bfloat16", "int32", "uint16", "float16"
_sb("ct", 4096)
_sb("ei", 256, I32); _sb("zi", 256, I32)
_sb("eo", 1280, U16); _sb("es", 1280, F16); _sb("zo", 1280, U16); _sb("zs", 1280, F16)
_sb("po", 1024, U16); _sb("ps", 768, F16)
_sb("pz", 256, F32); _sb("ef", 256, F32); _sb("yz", 256, F32)
CB = {}
for _n, _w in [("I", 128), ("nI", 128), ("I128", 128), ("p127", 128), ("p128", 128), ("m127", 128), ("m128", 128), ("m4096", 128), ("m64", 128),
               ("p32", 128), ("P2", 128), ("Sp", 128), ("ones", 128), ("c16", 128), ("cD", 128), ("cC", 256), ("neg", 128), ("pos", 128),
               ("keep", 128), ("b16", 16), ("b16x", 16)]:
    CB[_n] = (sum(w for _, w in CB.values()), _w)
_sb("cb", sum(w for _, w in CB.values()))
CF = {}
for _n in ("DA", "DB", "TC", "TS", "IV", "IF"):
    CF[_n] = (128 * len(CF), 128)
_sb("cf", 128 * len(CF), F32)
CH = {}
for _n, _w in [("b128", 16), ("b1", 16), ("I", 128), ("tri", 128), ("odd", 128)] + [(_x + _y, 128) for _y in "hl" for _x in ("DA", "DB", "TC", "TS")]:
    CH[_n] = (sum(w for _, w in CH.values()), _w)
_sb("ch", sum(w for _, w in CH.values()), F16)
_sb("b8", 8, F32)
_sb("col", 16, F32)
for _n, _w, _d in (("KI", 128, F32), ("KD", 128, F32), ("KT", 128, F32), ("UM", 128, F32), ("GG", 128, F32), ("t1", 128, F32),
                   ("t2", 128, F32), ("ki", 128, I32), ("pi", 2, I32), ("K8", 8, F32), ("u16f", 16, F32), ("f16", 16, F32), ("im16", 16, F32),
                   ("n80", 80, F32), ("n80i", 80, I32), ("w80", 80, F32), ("x80", 80, F32), ("a80", 80, F32)):
    _sb("k_" + _n, _w, _d)
for _h in range(NH):
    for _n, _w, _d in (("V", 2048, BF), ("Y", 2048, BF), ("cmp", 2048, BF), ("mx", 2048, BF), ("PA", 2048, F16), ("PB", 2048, F16), ("km", 128, F32),
                       ("r8", 8, F32), ("d", 128, BF), ("q1", 128, BF), ("q2", 128, BF), ("r", 128, F32), ("X", 128, BF), ("Mx", 128, BF),
                       ("Mn", 128, BF), ("LT", 128, BF), ("r16", 128, BF), ("hS", 128, BF), ("XA", 256, F16), ("XB", 256, F16), ("v", 128, I32),
                       ("S", 128, I32), ("cd", 128, I32), ("q", 128, F32), ("Zq", 128, F32), ("pr", 128, I32), ("F", 128, I32), ("m2", 128, F32),
                       ("val", 128, F32), ("del", 128, BF), ("E2", 128, BF), ("h2", 128, BF), ("EL", 128, BF), ("h", 128, F16),
                       ("AB", 256, F32), ("PP", 256, F32), ("fi", 128, F32), ("fm", 128, F32), ("w", 128, I32), ("pi", 128, I32), ("pf", 128, F16)):
        _sb("%s%d" % (_n, _h), _w, _d)
    for _n in "abcd":
        SCRATCH["ps%s%d" % (_n, _h)] = ("psum", [128, 512], F32)
SEMAPHORES += ["qP", "qV", "qS", "qG", "ld0", "ld1", "ld2", "snt", "out"]
for _t in range(1, RO + 1):
    for _h in range(NH):
        SEMAPHORES += ["%s%d%d" % (_k, _t, _h) for _k in ("eo", "es", "zo", "zs")]


def R(buf, c0, c1, step=1):
    return (buf, c0, c1, step)


def cb(n, lo=0, hi=None):
    c, w = CB[n]
    return R("cb", c + lo, c + (w if hi is None else hi))


def cf(n):
    c, w = CF[n]
    return R("cf", c, c + w)


def ch(n, w=None):
    return R("ch", CH[n][0], CH[n][0] + (w or CH[n][1]))


def ap(T, r):
    if r[3] == -1:
        return T[r[0]][:, r[2] - 1:r[1] - 1:-1] if r[1] else T[r[0]][:, r[2] - 1::-1]
    return T[r[0]][:, r[1]:r[2]:r[3]] if r[3] != 1 else T[r[0]][:, r[1]:r[2]]


def ncol(r):
    s = abs(r[3])
    return (r[2] - r[1] + s - 1) // s


def dts(r):
    return SCRATCH[r[0]][2]


def isp(r):
    return SCRATCH[r[0]][0] == "psum"


OPS, MARK = [], []


def op(eng, dur, fns, reads, writes, sem=None, inc=1, dep=None):
    OPS.append({"e": eng, "d": dur, "f": fns, "r": reads, "w": writes, "sem": sem, "inc": inc, "dep": dep})
    return len(OPS) - 1


def two(rs):
    return all(dts(r) in (BF, F16, U16) and not isp(r) for r in rs)


def cyc(n, x):
    return n * x * SC + FV


def ts(out, a, s1, op0, s2=None, op1=None):
    cols = [s for s in (s1, s2) if isinstance(s, tuple)]

    def f(g, T):
        x = ap(T, s1) if isinstance(s1, tuple) else s1
        y = ap(T, s2) if isinstance(s2, tuple) else s2
        if op1 is None:
            return g.vector.tensor_scalar(ap(T, out), ap(T, a), x, None, op0)
        return g.vector.tensor_scalar(ap(T, out), ap(T, a), x, y, op0, op1)
    return op("V", cyc(ncol(out), 0.5 if two([out, a]) else 1), [f], [a] + cols, [out])


def tt(out, a, b, o):
    return op("V", cyc(ncol(out), 1 if isp(a) or isp(b) else 2), [lambda g, T: g.vector.tensor_tensor(ap(T, out), ap(T, a), ap(T, b), o)], [a, b], [out])


def cp(out, a):
    return op("V", cyc(ncol(out), 0.5 if two([out, a]) else 1), [lambda g, T: g.vector.tensor_copy(ap(T, out), ap(T, a))], [a], [out])


def fill(out, c):
    return op("V", cyc(ncol(out), 0.5), [lambda g, T: g.vector.memset(ap(T, out), c)], [], [out])


def scan(out, d0, d1, o0, o1):
    return op("V", cyc(ncol(out), 0.5 if two([out, d0, d1]) else 1),
              [lambda g, T: g.vector.tensor_tensor_scan(ap(T, out), ap(T, d0), ap(T, d1), 0.0, o0, o1)], [d0, d1], [out])


def act(out, a, func, bias=None, scale=None):
    def f(g, T):
        kw = {}
        if bias is not None:
            kw["bias"] = bias
        if scale is not None:
            kw["scale"] = ap(T, scale) if isinstance(scale, tuple) else scale
        return g.scalar.activation(ap(T, out), ap(T, a), func, **kw)
    return op("S", ncol(out) * SC + FS, [f], [a] + ([scale] if isinstance(scale, tuple) else []), [out])


def gather(eng, out, offs):
    n = ncol(out)
    if eng == "S":
        f = lambda g, T: g.scalar.activation(ap(T, out), T["ct"][:, 0:4096].indirect(ap(T, offs)), AF.Copy)
    else:
        f = lambda g, T: g.vector.tensor_copy(ap(T, out), T["ct"][:, 0:4096].indirect(ap(T, offs)))
    return op(eng, n * GC * SC + 60, [f], [R("ct", 0, 4096), offs], [out])


def mm(lst):
    fns, rd, wr, d = [], [], [], 0.0
    for out, l, r, st, sp in lst:
        fns.append(lambda g, T, out=out, l=l, r=r, st=st, sp=sp: g.tensor.matmul(ap(T, out), ap(T, l), ap(T, r), st, sp))
        rd += [l, r]; wr.append(out)
        d += max(64, ncol(r)) * PC * (4 if dts(l) == F32 else 1)
    return op("P", d, fns, rd, wr)


def group(out, terms):
    return [(out, l, r, i == 0, i == len(terms) - 1) for i, (l, r) in enumerate(terms)]


def iota(out, pattern, base, cm):
    kw = {} if dts(out) == I32 else {"allow_small_or_imprecise_dtypes": True}
    return op("G", 130 + 2 * ncol(out) * SC, [lambda g, T: g.iota(ap(T, out), pattern, base, cm, **kw)], [], [out])


def constants():
    K = lambda n, w: R("k_" + n, 0, w)
    KI, KD, KT, UM, GG, t1, t2 = [K(n, 128) for n in ("KI", "KD", "KT", "UM", "GG", "t1", "t2")]
    ki, pi, K8 = K("ki", 128), K("pi", 2), K("K8", 8)
    col = lambda j: R("col", j, j + 1)
    iota(KI, [[-16, 8], [0, 16]], 0, 1)
    iota(KD, [[1, 128]], 0, -1)
    iota(K8, [[-16, 8]], 0, 1)
    iota(UM, [[0, 8], [1, 16]], 0, 0)
    iota(pi, [[0, 2]], 0, 1)
    iota(KT, [[16, 8], [1, 16]], 0, -1)
    for n, c in (("I", 1.0), ("nI", -1.0), ("I128", 1.0 / 128), ("p127", 127.0), ("p128", 128.0), ("m127", -127.0), ("m128", -128.0), ("m4096", -4096.0), ("m64", -32.0), ("p32", 16.0)):
        if n == "I":
            ts(cb(n), KD, 0.0, A.is_equal)
        else:
            act(cb(n), cb("I"), AF.Copy, scale=c)
    fill(cb("ones"), 1.0); fill(cb("c16"), 16.0); fill(cb("cC"), 0.0)
    ts(R("cb", CB["cC"][0], CB["cC"][0] + 128), UM, 0.0, A.is_equal, -1.0 / 128, A.mult)
    b8, t8 = R("b8", 0, 8), R("k_t1", 0, 8)
    ts(t8, K8, 0.0, A.is_ge)
    ts(b8, K8, 15.0, A.is_le)
    tt(b8, b8, t8, A.mult)
    for half in (0, 8):
        act(cb("b16", half, half + 8), b8, AF.Copy)
    act(cb("b16x", 0, 8), b8, AF.Copy, scale=16.0)
    ts(ch("b128", 8), b8, 128.0, A.mult)
    ts(ch("b1", 8), b8, 1.0, A.mult)
    cp(ch("I"), cb("I"))
    ts(GG, KI, 0.0, A.is_ge)
    ts(t1, KI, 15.0, A.is_le)
    tt(GG, GG, t1, A.mult)
    ts(t1, UM, 7.5, A.subtract, 1.0 / 128, A.mult)
    cp(cb("cD"), t1)
    ts(cb("neg"), UM, 0.0, A.is_equal, -1000.0, A.mult)
    ts(cb("pos"), UM, 0.0, A.is_equal, 1048576.0, A.mult)
    ts(cb("keep"), UM, 1.0, A.is_ge)
    cp(ki, KI)
    ts(ki, ki, 1, A.bitwise_and)
    tt(t1, ki, GG, A.mult)
    ts(ch("odd"), t1, -2.0, A.mult)
    ts(cb("P2"), KI, 15.0, A.is_equal)
    ts(t1, KD, 0.0, A.is_equal, 4096.0, A.mult)
    ts(t2, KD, -1.0, A.is_equal, 4096.0, A.mult)
    tt(t1, t1, t2, A.subtract)
    ts(t2, UM, 14.0, A.is_le)
    tt(cb("Sp"), t1, t2, A.mult)
    act(cf("IF"), cb("I"), AF.Copy)
    ts(t1, KT, 0.0, A.is_ge)
    tt(ch("tri"), t1, GG, A.mult)
    ts(pi, pi, 15, A.bitwise_and)
    ri = col(0)
    cp(ri, R("k_pi", 0, 1))
    ts(col(1), ri, 14.0, A.is_le, -4096.0, A.mult)
    ts(col(2), col(1), 960.0 + 16512.0 + 2048.0, A.add)
    ts(col(1), col(1), 127 * 7.5 + 96 - 129 - 16, A.add)
    ts(col(3), ri, 127.0, A.mult, -129.0, A.add)
    ts(col(4), ri, 128.0, A.mult, 16512.0, A.add)
    ts(col(5), ri, -1.0, A.mult, 16.0, A.add)
    u, f16, im = K("u16f", 16), K("f16", 16), K("im16", 16)
    cp(u, R("k_UM", 0, 16))
    ts(im, u, 9.0, A.is_ge)
    ts(f16, im, -8.0, A.mult)
    tt(f16, f16, u, A.add)
    ts(im, im, 4.0, A.mult)
    ts(col(6), ri, 9.0, A.is_ge)
    ts(col(7), col(6), -8.0, A.mult)
    tt(col(7), col(7), ri, A.add)
    ts(col(6), col(6), 4.0, A.mult)
    ts(col(8), col(7), 0.0, A.is_equal)
    ts(col(9), col(7), 8.0, A.is_equal)
    tt(col(8), col(8), col(9), A.add)
    ts(col(8), col(8), -1.0 / 16, A.mult, 2.0 / 16, A.add)
    n = lambda j: R("k_n80", 16 * j, 16 * j + 16)
    ts(n(2), f16, ri, A.mult)
    tt(n(0), n(2), im, A.add)
    ts(n(1), n(0), 4.0, A.add)
    ts(n(3), n(2), 12.0, A.add)
    ts(n(4), u, col(7), A.mult, col(6), A.add)
    N, NI, W, X2, AC = K("n80", 80), K("n80i", 80), K("w80", 80), K("x80", 80), K("a80", 80)
    cp(NI, N)
    ts(NI, NI, 15, A.bitwise_and)
    cp(N, NI)
    ts(W, N, -1.0, A.mult, 16.0, A.add)
    tt(W, W, N, A.min)
    ts(W, W, -1.0, A.mult, 4.0, A.add)
    tt(X2, W, W, A.mult)
    cc = [(-1) ** k * (math.pi / 8) ** (2 * k + 1) / math.factorial(2 * k + 1) for k in range(7)]
    ts(AC, X2, cc[6], A.mult, cc[5], A.add)
    for k in (4, 3, 2, 1, 0):
        tt(AC, AC, X2, A.mult)
        ts(AC, AC, cc[k], A.add)
    tt(AC, AC, W, A.mult)
    iv = R("k_a80", 64, 80)
    ts(iv, iv, col(8), A.mult)
    for j, name in enumerate(("DA", "DB", "TC", "TS", "IV")):
        c = CF[name][0]
        for q in range(8):
            act(R("cf", c + 16 * q, c + 16 * q + 16), R("k_a80", 16 * j, 16 * j + 16), AF.Copy, scale=R("b8", q, q + 1))
    hi, lo = R("ch", CH["DAh"][0], CH["DAh"][0] + 512), R("ch", CH["DAl"][0], CH["DAl"][0] + 512)
    cp(hi, R("cf", 0, 512))
    tt(lo, R("cf", 0, 512), hi, A.subtract)


M4, M16 = 1.5 * 2 ** 25, 1.5 * 2 ** 27


def half_round(t, h, hop):
    MARK.append((len(OPS), 2 * t + h))
    b = lambda n, lo=0, hi=128: R("%s%d" % (n, h), lo, hi)
    pa, pb, pc, pd = ["ps%s%d" % (x, h) for x in "abcd"]
    q = lambda p, j, k=1: R(p, 128 * j, 128 * (j + k))
    o = 256 * (t - 1) + 128 * h
    eo, es, zo, zs = R("eo", o, o + 128), R("es", o, o + 128), R("zo", o, o + 128), R("zs", o, o + 128)
    col = lambda j: R("col", j, j + 1)
    hop(t, h, "z")
    for buf, ls, cuts in (("V", (eo[0], eo[1]), VCUT), ("Y", (zo[0], zo[1]), YCUT)):
        c = 0
        for eng, w in cuts:
            gather(eng, b(buf, 16 * c, 16 * (c + w)), R(ls[0], ls[1] + c, ls[1] + c + w))
            c += w
    ts(b("hS"), es, 2048 + 16448.5, A.add)
    v15 = R("V%d" % h, 15, 2048, 16)
    for c in range(0, 16 - NV, 4):
        for j in range(4):
            mm(group(q(pd, j), [(cb("I"), R("Y%d" % h, c + j, 2048, 16)), (cb("nI"), v15)]))
        act(b("mx", 128 * c, 128 * c + 512), q(pd, 0, 4), AF.Abs)
    if NV:
        mm([(q(pc, 0), cb("I"), v15, True, True)])
        for p in range(16 - NV, 16):
            tt(b("mx", 128 * p, 128 * p + 128), R("Y%d" % h, p, 2048, 16), q(pc, 0), A.subtract)
        for p in range(16 - NV, 16, 4):
            x = b("mx", 128 * p, 128 * min(16, p + 4))
            act(x, x, AF.Abs)
    mm([(q(pd, 1), cb("ones"), cb("cD"), True, False)])
    for p in range(16):
        mm([(R(pd, 128 + p, 256, 16), b("mx", 128 * p, 128 * p + 128), cb("b16x", 0, 8), False, p == 15)])
    scan(b("km"), cb("pos"), q(pd, 1), A.add, A.min)
    km = R("km%d" % h, 15, 128, 16)
    ts(b("r8", 0, 8), km, M16, A.add, M16, A.subtract)
    for c in range(4):
        bank = pa if c % 2 == 0 else pb
        for j in range(4):
            k = 4 * c + j
            mm(group(q(bank, j), [(cb("I"), R("V%d" % h, k, 2048, 16)), (cb("nI"), R("V%d" % h, (k + 1) % 16, 2048, 16))]))
        act(b("cmp", 512 * c, 512 * c + 512), q(bank, 0, 4), AF.Sign, -0.5)
    mm([(q(pa, 0, 2), cb("ones"), cb("cC"), True, False)] + ([(q(pa, 1), b("h"), ch("odd"), False, False)] if t > 1 else []))
    for k in range(0, 16, 4):
        mm([(R(pa, j, 256, 16), b("cmp", 128 * j, 128 * j + 128), cb("b16"), False, j == 15) for j in range(k, k + 4)])
    act(b("q1"), q(pa, 1), AF.Sign, 5.0)
    act(b("q2"), q(pa, 0), AF.Sign, -2.5)
    scan(q(pc, 0), cb("keep"), q(pa, 0), A.mult, A.add)
    ts(b("r"), q(pc, 0), M4, A.add, M4, A.subtract)
    tt(b("d"), b("r"), q(pc, 0), A.subtract)
    tt(R("d%d" % h, 0, 128, 16), km, b("r8", 0, 8), A.subtract)
    scan(b("X"), cb("keep"), b("d"), A.mult, A.add)
    rev = lambda n: R("%s%d" % (n, h), 0, 128, -1)
    scan(rev("Mx"), cb("neg"), rev("X"), A.add, A.max)
    scan(rev("Mn"), cb("pos"), rev("X"), A.add, A.min)
    ts(b("r16"), b("X"), M16, A.add, M16, A.subtract)
    mm(group(q(pb, 0), [(b("Mx"), cb("I")), (b("Mn"), cb("nI"))]))
    act(b("LT"), q(pb, 0), AF.Copy)
    XA, XB = q(pc, 1), q(pd, 2)
    mm([(XA, b("q1"), cb("m64"), True, False), (XA, b("q2"), cb("p32"), False, False), (XA, cb("I128"), b("hS"), False, False)])
    mm([(XB, ch("I"), es, True, False), (XB, cb("nI"), b("hS"), False, False)])
    mm([(XA, b("X"), cb("p127"), False, False), (XA, b("r16"), cb("m127"), False, False)])
    mm([(XB, b("X"), cb("p128"), False, False), (XB, b("r16"), cb("m128"), False, False)])
    mm([(XA, cb("Sp"), b("LT"), False, True)])
    mm([(XB, cb("Sp"), b("LT"), False, True)])

    def keys(ka, kb, ca, cc):
        ts(b("XA"), ka, ca, A.add)
        ts(b("XA", 128, 256), ka, ca, A.add, -8 * 127.0, A.add)
        ts(b("XB"), kb, cc, A.add)
        ts(b("XB", 128, 256), kb, cc, A.add, -8 * 128.0, A.add)

    def route(bank):
        for p in range(8):
            ts(b("PA", 256 * p, 256 * p + 256), b("XA", 0, 256), 127.0 * p, A.max, 127.0 * (p + 1), A.min)
            ts(b("PB", 256 * p, 256 * p + 256), b("XB", 0, 256), 128.0 * p, A.max, 128.0 * (p + 1), A.min)
            for k in (0, 1):
                c = 256 * p + 128 * k
                mm(group(R(bank, p + 8 * k, 128, 16), [(b("PA", c, c + 128), ch("b128", 8)), (b("PB", c, c + 128), ch("b1", 8))]))

    keys(XA, XB, col(1), col(2))
    mm(group(q(pc, 2), [(ch("DAh"), es), (ch("DAl"), es)]) + group(q(pc, 3), [(ch("DBh"), es), (ch("DBl"), es)]))
    act(b("AB", 0, 256), q(pc, 2, 2), AF.Copy)
    mm(group(q(pa, 0), [(zs, ch("I")), (cb("ones"), cb("c16"))]))
    route(pd)
    cp(b("v"), q(pd, 0))
    ts(b("S"), b("v"), 4095, A.bitwise_and)
    ts(b("cd"), b("v"), 12, A.arith_shift_right, 3, A.bitwise_and)
    tt(b("pr"), b("S"), q(pa, 0), A.mult)
    ts(b("del"), b("cd"), 3.0, A.is_ge)
    ts(b("F"), b("pr"), 5, A.arith_shift_right, 4095, A.bitwise_and)
    ts(q(pa, 1), b("cd"), 2.0, A.is_ge)
    scan(b("E2"), cb("keep"), b("del"), A.mult, A.add)
    ts(q(pa, 2), b("cd"), 2.0, A.is_ge, 77.0 * t, A.mult)
    ts(b("q"), b("cd"), 0.0, A.is_equal)
    tt(b("m2"), b("S"), q(pa, 2), A.add)
    tt(q(pa, 3), b("q"), q(pa, 0), A.mult)
    tt(q(pa, 2), b("m2"), q(pa, 3), A.add)
    tt(b("Zq"), b("F"), q(pa, 1), A.mult)
    tt(b("val"), b("Zq"), q(pa, 2), A.add)
    act(b("h2"), b("val"), AF.Identity, 16448.5)
    XA, XB = q(pb, 0), q(pc, 2)
    mm([(XA, b("E2"), cb("m127"), True, False), (XA, b("del"), cb("m4096"), False, False)])
    mm([(XB, b("E2"), cb("m128"), True, False), (XB, b("del"), cb("m4096"), False, False)])
    mm(group(q(pd, 3), [(b("E2"), cb("I"))]))
    act(b("EL"), q(pd, 3), AF.Copy)
    mm(group(q(pd, 2), [(cb("P2"), b("EL"))]))
    ts(b("h"), q(pd, 2), col(5), A.is_equal)
    mm([(XB, b("val"), cf("IF"), False, False)])
    mm([(XA, b("h2"), cb("I128"), False, True)])
    mm([(XB, b("h2"), cb("nI"), False, True)])
    keys(XA, XB, col(3), col(4))
    mm(group(q(pd, 0), [(ch("TCh"), b("h")), (ch("TCl"), b("h"))]) + group(q(pd, 1), [(ch("TSh"), b("h")), (ch("TSl"), b("h"))]) +
       group(q(pd, 2), [(b("h"), ch("tri"))]))
    tt(b("PP", 0, 256), b("AB", 0, 256), q(pd, 0, 2), A.mult)
    mm(group(q(pc, 0), [(b("PP", 0, 128), cf("IV")), (b("PP", 128, 256), cf("IV"))]))
    act(b("fi"), q(pc, 0), AF.Copy, 2048.0)
    tt(b("fm"), b("fi"), q(pd, 2), A.mult)
    route(pb)
    tt(b("w"), b("fm"), q(pb, 0), A.add)
    ts(b("pi"), b("w"), 4095, A.bitwise_and)
    ts(b("pf"), b("pi"), -2048.0, A.add)
    mm(group(q(pa, 0), [(b("pf"), ch("I"))]))
    if t < RO:
        ts(R("po", o, o + 128), q(pa, 0), 2048.0, A.add)
        cp(R("ps", o, o + 128), q(pa, 0))
    else:
        act(R("pz", 128 * h, 128 * h + 128), q(pa, 0), AF.Copy, 2048.0)
    hop(t, h, "e")


def build():
    def load(q, sem, dst, src):
        op(q, 60, [lambda g, T: g.sync.dma_start(ap(T, dst), T[src][:])], [], [("dma_" + sem, 0, 1, 1)])
        op("X", 2500, [], [("dma_" + sem, 0, 1, 1)], [dst], sem=sem, inc=16)

    load("Y", "ld0", R("ei", 0, 256), "enz")
    load("Y", "ld1", R("ct", 0, 4096), "cont")
    load("Y", "ld2", R("zi", 0, 256), "subs")

    def send(dst_of, src, dst, sem):
        def f(g, T, core, topo):
            to = T.cores[(T.rank_of(core) + dst_of) % len(T.cores)]
            rid, pid, _ = topo.addr(to)
            m = sum(1 << e for e in topo.engines(core, to))
            g.remote_dma(ap(T, dst), ap(T, src), T.sem[sem], T.sem.snt, pid, rid, m)
            return bin(m).count("1")
        op("R", 1000, [f], [src], [("net_" + sem, 0, 1, 1)])
        op("X", NET, [], [("net_" + sem, 0, 1, 1)], [dst], sem=sem, inc=8)

    def hop(t, h, kind):
        o = 256 * (t - 1) + 128 * h
        n = o + 256
        for x in ("o", "s"):
            if x == "o" and t == RO:
                continue
            s = (kind + x if kind == "z" else kind + x) + "%d%d" % (t, h)
            src = ("e" + x) if kind == "z" else ("p" + x)
            if kind == "e" and t == RO:
                send(2, R("pz", 128 * h, 128 * h + 128), R("ef", 128 * h, 128 * h + 128), s)
            else:
                send(1 if kind == "z" else 2, R(src, o, o + 128), R(kind + x, n, n + 128), s)

    for k in "ez":
        for h in range(NH):
            c = R(k + "i", 128 * h, 128 * h + 128)
            cp(R(k + "o", 128 * h, 128 * h + 128), c)
            ts(R(k + "s", 128 * h, 128 * h + 128), c, -2048.0, A.add)
    constants()
    for t in range(1, RO + 1):
        for h in range(NH):
            half_round(t, h, hop)
    o = 256 * RO
    for h in range(NH):
        ts(R("yz", 128 * h, 128 * h + 128), R("zs", o + 128 * h, o + 128 * h + 128), 2048.0, A.add)
    for src, dst in (("yz", "ysub"), ("ef", "yenz")):
        for h in range(NH):
            op("Y", 60, [lambda g, T, src=src, dst=dst, h=h: g.sync.dma_start(T[dst][:, 128 * h:128 * h + 128], T[src][:, 128 * h:128 * h + 128])],
               [R(src, 128 * h, 128 * h + 128)], [], sem="out", inc=16)


def analyse():
    hist = {}
    for i, x in enumerate(OPS):
        deps = {}
        if x["dep"] is not None:
            deps[x["dep"]] = True
        acc = [(r, False) for r in x["r"]] + [(w, True) for w in x["w"]]
        for (buf, lo, hi, stp), wr in acc:
            psum = buf in SCRATCH and SCRATCH[buf][0] == "psum"
            for (l2, h2, s2, w2, j) in hist.get(buf, []):
                over = lo < h2 and l2 < hi
                y = OPS[j]
                if over and stp == s2 and stp > 1 and (lo - l2) % stp != 0:
                    over = False
                if psum and y["e"] != x["e"]:
                    deps[j] = True
                elif psum and x["e"] == "P":
                    deps[j] = deps.get(j, False)
                elif over and w2 and not wr:
                    deps[j] = True
                elif over and (wr or w2):
                    deps[j] = deps.get(j, False) or y["e"] != x["e"] or x["e"] != "P"
        x["deps"] = deps
        for (buf, lo, hi, stp), wr in acc:
            lst = hist.setdefault(buf, [])
            psum = buf in SCRATCH and SCRATCH[buf][0] == "psum"
            if wr and stp == 1:
                lst[:] = [e for e in lst if not (lo <= e[0] and e[1] <= hi and not (psum and OPS[e[4]]["e"] != x["e"] and False)) or e[4] == i]
            if psum and wr and x["e"] == "P" and lo == 0 and False:
                lst.clear()
            lst.append((lo, hi, stp, wr, i))
            if psum:
                while len(lst) > 400:
                    lst.pop(0)


def schedule(rw=RW, bonus=BONUS):
    n = len(OPS)
    rk = [0] * n
    for (a, k), (z, _) in zip(MARK, MARK[1:] + [(n, 0)]):
        for i in range(a, z):
            rk[i] = k
    succ, nd = [[] for _ in range(n)], [0] * n
    for i, x in enumerate(OPS):
        nd[i] = len(x["deps"])
        for j in x["deps"]:
            succ[j].append(i)
    path = [0.0] * n
    for i in range(n - 1, -1, -1):
        path[i] = OPS[i]["d"] + max([path[s] + LAG for s in succ[i]], default=0.0)
        if rk[i] == 0:
            rk[i] = min([rk[s] for s in succ[i]], default=99)
    pri = [path[i] - rw * rk[i] + bonus.get(OPS[i]["w"][0][0][:-1] if OPS[i]["w"] else "", 0.0) for i in range(n)]
    ready, t0, free, order, end = {}, [0.0] * n, {}, [], [0.0] * n
    for i in range(n):
        if nd[i] == 0:
            ready.setdefault(OPS[i]["e"], set()).add(i)
    while len(order) < n:
        best = None
        for e, s in ready.items():
            f = 0.0 if e == "X" else free.get(e, 0.0)
            for i in s:
                k = (max(f, t0[i]), -pri[i], i)
                if best is None or k < best[0]:
                    best = (k, i, e)
        (st, _, _), i, e = best
        ready[e].discard(i)
        end[i] = st + OPS[i]["d"]
        if e != "X":
            free[e] = end[i]
        order.append(i)
        for s in succ[i]:
            t0[s] = max(t0[s], end[i] + (LAG if OPS[s]["deps"][i] else 0.0))
            nd[s] -= 1
            if nd[s] == 0:
                ready.setdefault(OPS[s]["e"], set()).add(s)
    return order, max(end)


PLAN = []


def plan():
    if not PLAN:
        build()
        analyse()
        order, tot = schedule()
        PLAN.append(order)
        PLAN.append(tot)
    return PLAN[0]


QS = {"P": "qP", "V": "qV", "S": "qS", "G": "qG"}


def rank_program(g, core, T, topo):
    if T.rank_of(core) is None:
        return
    order = plan()
    queue = {"P": g.tensor, "V": g.vector, "S": g.scalar, "G": g, "R": g, "Y": g.sync}
    qname = {"G": "g", "R": "g"}
    cnt, done, know, clock, sent = {}, {}, {}, {}, 0
    for i in order:
        x = OPS[i]
        e = x["e"]
        if e == "X":
            done[i] = (x["sem"], x["inc"])
            clock[i] = {}
            continue
        qn = qname.get(e, e)
        kn = know.setdefault(qn, {})
        need = {}
        for j, w in x["deps"].items():
            if w and done.get(j) is not None:
                s, v = done[j]
                if need.get(s, (0, 0))[0] < v:
                    need[s] = (v, j)
        for s, (v, j) in sorted(need.items(), key=lambda z: -z[1][1]):
            if kn.get(s, 0) >= v:
                continue
            queue[e].wait_ge(T.sem[s], v)
            for s2, v2 in clock[j].items():
                kn[s2] = max(kn.get(s2, 0), v2)
            kn[s] = max(kn.get(s, 0), v)
        clock[i] = dict(kn)
        if e in QS:
            s = QS[e]
            for f in x["f"]:
                f(g, T).then_inc(T.sem[s], 1)
                cnt[s] = cnt.get(s, 0) + 1
            done[i] = (s, cnt[s])
        elif e == "R":
            for f in x["f"]:
                sent += f(g, T, core, topo)
            done[i] = None
        else:
            sem = x["sem"]
            if sem is None:
                sem = OPS[i]["w"][0][0][4:]
            for f in x["f"]:
                f(g, T).then_inc(T.sem[sem], 16)
                cnt[sem] = cnt.get(sem, 0) + 16
            done[i] = None
    for s in list(QS.values()) + ["out", "ld0", "ld1", "ld2"]:
        if cnt.get(s, 0):
            g.sync.wait_ge(T.sem[s], cnt[s])
    g.wait_ge(T.sem.snt, sent)
